import numpy as np
import ml_dtypes


def mxq(x, axis, fmt="e4m3"):
    dtype, down = {"e4m3": (ml_dtypes.float8_e4m3fn, 7), "e5m2": (ml_dtypes.float8_e5m2, 14)}[fmt]
    v = np.moveaxis(np.asarray(x, np.float32).astype(ml_dtypes.bfloat16).astype(np.float64), axis, -1)
    blocks = v.reshape(v.shape[:-1] + (-1, 32))
    amax = np.abs(blocks).max(-1, keepdims=True)
    byte = np.maximum(np.where(amax > 0, np.frexp(amax)[1] - 1 + 127, 0) - down, 1)
    scale = np.exp2(byte - 127.0)
    codes = (blocks / scale).astype(np.float32).astype(dtype).astype(np.float64)
    return np.moveaxis((codes * scale).reshape(v.shape), -1, axis)


WIDE = False


def mx_kscale(k):
    if not WIDE:
        return np.ones(k)
    levels = np.array([10, -10, 5, -5, 0])
    if k % 512:
        return np.exp2(np.random.permutation(np.resize(levels, k // 32))).repeat(32)
    a = np.empty((k // 512, 16))
    for p in range(k // 512):
        a[p, :8] = np.random.permutation(np.resize(levels, 8))
        for g in range(8):
            far = levels[np.abs(levels - a[p, g]) >= 10]
            a[p, g + 8] = far[np.random.randint(len(far))]
    return np.exp2(a.ravel()).repeat(32)


def f64(x):
    return np.asarray(x).astype(np.float64)


def striped(idx):
    return np.tile(np.asarray(idx).reshape(-1, 16).T, (8, 1)).astype(np.uint16)


def unstriped(offs):
    return offs[:16].T.reshape(-1).astype(np.int64)

def silu(v):
    return v / (1.0 + np.exp(-v))


def bf(x):
    return np.asarray(x, np.float32).astype(ml_dtypes.bfloat16)


def planes(Y):
    r, m = Y.shape
    b = f64(bf(Y)).reshape(r // 32, 32, m)
    amax = np.abs(b).max(1)
    byte = np.clip(np.where(amax > 0, np.frexp(amax)[1] - 1 + 127 - 7, 1), 1, 254)
    codes = (b * np.exp2(127.0 - byte)[:, None, :]).reshape(r, m).astype(np.float32).astype(ml_dtypes.float8_e4m3fn).view(np.uint8)
    words = codes.reshape(r // 512, 128, 4, m).transpose(0, 1, 3, 2)
    return np.ascontiguousarray(words), np.ascontiguousarray(byte.astype(np.uint8).reshape(r // 512, 16, m))


B, N, T, D, NQ = 1, 512, 2048, 512, 512
DV = 512


def setup_inputs():
    n = np.random.standard_normal
    idx = np.random.permutation(T)[:B * N]
    u = mx_kscale(N)
    ut = np.ones(T)
    ut[idx] = u
    return {
        "vT": (n((DV, T)) / ut).astype(np.float32),
        "wT": (np.random.dirichlet(np.ones(N), NQ).T[None] * u[:, None] * 16).astype(np.float32),
        "gn": (np.random.uniform(0.5, 2.0, (B, DV, 1))).astype(np.float32),
        "offs": striped(idx),
    }


def reference(vT, wT, gn, offs):
    idx = unstriped(offs)
    pick = lambda x, which: x[:, which].reshape(x.shape[0], B, -1).transpose(1, 0, 2)
    wq = mxq(f64(wT), 1, "e4m3")
    o = mxq(pick(f64(vT), idx).transpose(0, 2, 1), 1, "e4m3").transpose(0, 2, 1) @ wq
    r_ = silu(o * f64(gn))
    Y = r_[0]
    words, scales = planes(Y)
    return Y, words, scales

@@ -1,0 +1,157 @@
+from contextlib import ExitStack
+
+import concourse.mybir as mybir
+from concourse.masks import make_identity
+
+F32 = mybir.dt.float32
+BF16 = mybir.dt.bfloat16
+I32 = mybir.dt.int32
+U32 = mybir.dt.uint32
+U16 = mybir.dt.uint16
+U8 = mybir.dt.uint8
+FP8X4 = mybir.dt.float8_e4m3fn_x4
+SILU = mybir.ActivationFunctionType.Silu
+
+P = 128
+PACK = 4
+SLOTS = 512
+TOKENS = 2048
+QUERIES = 512
+HALF = QUERIES // 2
+
+FLOPS = 2 * 512 * 512 * 512
+
+
+def tile_attend_plo_wsum_f_topk_kernel(tc, vT, wT, gn, offs, out_0, out_1, out_2):
+    nc = tc.nc
+    v_rows = vT.rearrange("(p t) n -> p t n", t=PACK)
+    w_rows = wT[0].rearrange("(p j) q -> p j q", j=PACK)
+    y_rows = out_0.rearrange("(p t) q -> p t q", t=PACK)
+    y_words = out_1[0].rearrange("p q u -> p (q u)").bitcast(I32)
+    y_scale_rows = out_2[0].bitcast(I32)
+
+    with ExitStack() as ctx:
+        keep = ctx.enter_context(tc.tile_pool(name="keep", bufs=1))
+        turn = ctx.enter_context(tc.psum_pool(name="turn", bufs=2))
+        sums = ctx.enter_context(tc.psum_pool(name="sums", bufs=6))
+
+        offsets = keep.tile([P, SLOTS // 16], U16, name="offsets")
+        gains = keep.tile([P, PACK], F32, name="gains")
+        pools = [keep.tile([P, TOKENS], F32, name=f"pool{t}") for t in range(PACK)]
+        w_raw = [keep.tile([P, PACK, HALF], F32, name=f"w_raw{h}") for h in range(2)]
+
+        nc.sync.dma_start(out=pools[0][:], in_=v_rows[:, 0, :])
+        nc.sync.dma_start(offsets[:], offs)
+        nc.sync.dma_start(out=gains[:], in_=gn[0].rearrange("(p t) o -> p (t o)", t=PACK))
+        nc.sync.dma_start(out=w_raw[0][:], in_=w_rows[:, :, 0:HALF])
+        for t in range(1, PACK):
+            nc.sync.dma_start(out=pools[t][:], in_=v_rows[:, t, :])
+        nc.sync.dma_start(out=w_raw[1][:], in_=w_rows[:, :, HALF:QUERIES])
+
+        identity = keep.tile([P, P], F32, name="identity")
+        make_identity(nc, identity[:])
+
+        v_codes = [keep.tile([P, P], U32, name=f"v_codes{t}", align_bytes=64) for t in range(PACK)]
+        v_scales = [keep.tile([P, P], U8, name=f"v_scales{t}", align_bytes=64) for t in range(PACK)]
+        w_codes = [keep.tile([P, HALF], U32, name=f"w_codes{h}", align_bytes=64) for h in range(2)]
+        w_scales = [keep.tile([P, HALF], U8, name=f"w_scales{h}", align_bytes=64) for h in range(2)]
+        w_grouped = [keep.tile([P, HALF, PACK], BF16, name=f"w_grouped{h}", align_bytes=64) for h in range(2)]
+        v_grouped = [keep.tile([P, P, PACK], BF16, name=f"v_grouped{t}", align_bytes=64) for t in range(PACK)]
+        y = [[keep.tile([P, 2, HALF], F32, name=f"y{h}{u}") for u in range(2)] for h in range(2)]
+        y_grouped = [keep.tile([P, HALF, PACK], BF16, name=f"y_grouped{h}", align_bytes=64) for h in range(2)]
+        y_codes = [keep.tile([P, HALF], U32, name=f"y_codes{h}", align_bytes=64) for h in range(2)]
+        y_scales = keep.tile([P, QUERIES], U8, name="y_scales", align_bytes=64)
+
+        def group_weights(h):
+            nc.vector.tensor_copy(
+                out=w_grouped[h][:].rearrange("p (c i) j -> p c j i", i=4),
+                in_=w_raw[h][:].rearrange("p j (c i) -> p c j i", i=4),
+            )
+
+        def quantize_weights(h):
+            nc.vector.quantize_mx(
+                out=w_codes[h][:].bitcast(FP8X4),
+                scales=w_scales[h][:],
+                in_=w_grouped[h][:].rearrange("p q j -> p (q j)"),
+            )
+
+        def gather_and_turn(t):
+            picked = keep.tile([P, SLOTS], BF16, name=f"picked{t}", align_bytes=64)
+            nc.vector.tensor_copy(picked[:], pools[t][:].indirect(offsets[:]))
+            pairs = picked[:].bitcast(F32)
+            turned = turn.tile([P, 2, P], F32, name="turned")
+            for u in range(2):
+                nc.tensor.transpose(turned[:, u, :], pairs[:, u : SLOTS // 2 : 2], identity[:])
+            nc.scalar.copy(
+                out=v_grouped[t][:].rearrange("s m j -> s (m j)").bitcast(F32).rearrange("s (m u) -> s m u", u=2),
+                in_=turned[:].rearrange("s u m -> s m u"),
+            )
+
+        def quantize_values(t):
+            nc.vector.quantize_mx(
+                out=v_codes[t][:].bitcast(FP8X4),
+                scales=v_scales[t][:],
+                in_=v_grouped[t][:].rearrange("s m j -> s (m j)"),
+            )
+
+        def multiply(t, h):
+            acc = sums.tile([P, HALF], F32, name="acc")
+            nc.tensor.matmul_mx(
+                out=acc[:],
+                lhsT=v_codes[t][:].bitcast(FP8X4),
+                lhsT_scale=v_scales[t][:],
+                rhs=w_codes[h][:].bitcast(FP8X4),
+                rhs_scale=w_scales[h][:],
+                start=True,
+                stop=True,
+            )
+            nc.scalar.activation(out=y[h][t // 2][:, t % 2, :], in_=acc[:], func=SILU, scale=gains[:, t : t + 1])
+
+        def hand_out_pair(h, u):
+            cols = slice(h * HALF, (h + 1) * HALF)
+            nc.sync.dma_start(out=y_rows[:, 2 * u : 2 * u + 2, cols], in_=y[h][u][:])
+            nc.vector.tensor_copy(
+                out=y_grouped[h][:, :, 2 * u : 2 * u + 2].rearrange("p (c i) e -> p c e i", i=4),
+                in_=y[h][u][:].rearrange("p e (c i) -> p c e i", i=4),
+            )
+
+        def quantize_result(h):
+            cols = slice(h * HALF, (h + 1) * HALF)
+            nc.vector.quantize_mx(
+                out=y_codes[h][:].bitcast(FP8X4),
+                scales=y_scales[:, cols],
+                in_=y_grouped[h][:].rearrange("p q t -> p (q t)"),
+            )
+            nc.sync.dma_start(out=y_words[:, cols], in_=y_codes[h][:].bitcast(I32))
+
+        gather_and_turn(0)
+        group_weights(0)
+        quantize_values(0)
+        quantize_weights(0)
+        multiply(0, 0)
+        for t in (1, 2):
+            gather_and_turn(t)
+            quantize_values(t)
+            multiply(t, 0)
+            if t == 1:
+                hand_out_pair(0, 0)
+        gather_and_turn(3)
+        group_weights(1)
+        quantize_values(3)
+        quantize_weights(1)
+        multiply(3, 0)
+        multiply(0, 1)
+        multiply(1, 1)
+        hand_out_pair(0, 1)
+        quantize_result(0)
+        hand_out_pair(1, 0)
+        multiply(2, 1)
+        multiply(3, 1)
+        hand_out_pair(1, 1)
+        quantize_result(1)
+        for quad in range(4):
+            queue = nc.scalar if quad % 2 == 0 else nc.sync
+            queue.dma_start(
+                out=y_scale_rows[4 * quad : 4 * quad + 4, :],
+                in_=y_scales[32 * quad : 32 * quad + 4, :].bitcast(I32),
+            )

@@ -19,6 +19,9 @@ TOKENS = 2048
 QUERIES = 512
 HALF = QUERIES // 2
 
+SCALAR_COLS = 96
+POOL_BYTES = 4 * TOKENS
+
 FLOPS = 2 * 512 * 512 * 512
 
 
@@ -32,40 +35,43 @@ def tile_attend_plo_wsum_f_topk_kernel(tc, vT, wT, gn, offs, out_0, out_1, out_2
 
     with ExitStack() as ctx:
         keep = ctx.enter_context(tc.tile_pool(name="keep", bufs=1))
+        late = ctx.enter_context(tc.tile_pool(name="late", bufs=1))
         turn = ctx.enter_context(tc.psum_pool(name="turn", bufs=2))
         sums = ctx.enter_context(tc.psum_pool(name="sums", bufs=6))
 
         offsets = keep.tile([P, SLOTS // 16], U16, name="offsets")
         gains = keep.tile([P, PACK], F32, name="gains")
-        pools = [keep.tile([P, TOKENS], F32, name=f"pool{t}") for t in range(PACK)]
-        w_raw = [keep.tile([P, PACK, HALF], F32, name=f"w_raw{h}") for h in range(2)]
+        pools = [late.tile([P, TOKENS], F32, name=f"pool{t}", align_bytes=64, offset=t * POOL_BYTES) for t in range(PACK)]
+        w_raw = [late.tile([P, PACK, HALF], F32, name=f"w_raw{h}", align_bytes=64, offset=(PACK + h) * POOL_BYTES) for h in range(2)]
 
         nc.sync.dma_start(out=pools[0][:], in_=v_rows[:, 0, :])
         nc.sync.dma_start(offsets[:], offs)
         nc.sync.dma_start(out=gains[:], in_=gn[0].rearrange("(p t) o -> p (t o)", t=PACK))
+        nc.sync.dma_start(out=pools[1][:], in_=v_rows[:, 1, :])
         nc.sync.dma_start(out=w_raw[0][:], in_=w_rows[:, :, 0:HALF])
-        for t in range(1, PACK):
-            nc.sync.dma_start(out=pools[t][:], in_=v_rows[:, t, :])
+        nc.sync.dma_start(out=pools[2][:], in_=v_rows[:, 2, :])
+        nc.sync.dma_start(out=pools[3][:], in_=v_rows[:, 3, :])
         nc.sync.dma_start(out=w_raw[1][:], in_=w_rows[:, :, HALF:QUERIES])
 
         identity = keep.tile([P, P], F32, name="identity")
         make_identity(nc, identity[:])
 
-        v_codes = [keep.tile([P, P], U32, name=f"v_codes{t}", align_bytes=64) for t in range(PACK)]
+        v_codes = {}
         v_scales = [keep.tile([P, P], U8, name=f"v_scales{t}", align_bytes=64) for t in range(PACK)]
         w_codes = [keep.tile([P, HALF], U32, name=f"w_codes{h}", align_bytes=64) for h in range(2)]
         w_scales = [keep.tile([P, HALF], U8, name=f"w_scales{h}", align_bytes=64) for h in range(2)]
-        w_grouped = [keep.tile([P, HALF, PACK], BF16, name=f"w_grouped{h}", align_bytes=64) for h in range(2)]
-        v_grouped = [keep.tile([P, P, PACK], BF16, name=f"v_grouped{t}", align_bytes=64) for t in range(PACK)]
+        w_grouped = [late.tile([P, HALF, PACK], BF16, name=f"w_grouped{h}", align_bytes=64, offset=(9 + h) * POOL_BYTES) for h in range(2)]
+        v_grouped = {}
+        turned = {}
         y = [[keep.tile([P, 2, HALF], F32, name=f"y{h}{u}") for u in range(2)] for h in range(2)]
-        y_grouped = [keep.tile([P, HALF, PACK], BF16, name=f"y_grouped{h}", align_bytes=64) for h in range(2)]
+        y_grouped = {}
         y_codes = [keep.tile([P, HALF], U32, name=f"y_codes{h}", align_bytes=64) for h in range(2)]
         y_scales = keep.tile([P, QUERIES], U8, name="y_scales", align_bytes=64)
 
-        def group_weights(h):
-            nc.vector.tensor_copy(
-                out=w_grouped[h][:].rearrange("p (c i) j -> p c j i", i=4),
-                in_=w_raw[h][:].rearrange("p j (c i) -> p c j i", i=4),
+        def group_weights(copy, h, cols):
+            copy(
+                out=w_grouped[h][:, cols, :].rearrange("p (c i) j -> p c j i", i=4),
+                in_=w_raw[h][:, :, cols].rearrange("p j (c i) -> p c j i", i=4),
             )
 
         def quantize_weights(h):
@@ -79,15 +85,19 @@ def tile_attend_plo_wsum_f_topk_kernel(tc, vT, wT, gn, offs, out_0, out_1, out_2
             picked = keep.tile([P, SLOTS], BF16, name=f"picked{t}", align_bytes=64)
             nc.vector.tensor_copy(picked[:], pools[t][:].indirect(offsets[:]))
             pairs = picked[:].bitcast(F32)
-            turned = turn.tile([P, 2, P], F32, name="turned")
+            turned[t] = turn.tile([P, 2, P], F32, name="turned")
             for u in range(2):
-                nc.tensor.transpose(turned[:, u, :], pairs[:, u : SLOTS // 2 : 2], identity[:])
+                nc.tensor.transpose(turned[t][:, u, :], pairs[:, u : SLOTS // 2 : 2], identity[:])
+
+        def group_values(t):
+            v_grouped[t] = late.tile([P, P, PACK], BF16, name=f"v_grouped{t}", align_bytes=64, offset=(6, 7, 8, 5)[t] * POOL_BYTES + 1024)
             nc.scalar.copy(
                 out=v_grouped[t][:].rearrange("s m j -> s (m j)").bitcast(F32).rearrange("s (m u) -> s m u", u=2),
-                in_=turned[:].rearrange("s u m -> s m u"),
+                in_=turned[t][:].rearrange("s u m -> s m u"),
             )
 
         def quantize_values(t):
+            v_codes[t] = late.tile([P, P], U32, name=f"v_codes{t}", align_bytes=64, offset=(1, 11, 5, 10)[t] * POOL_BYTES)
             nc.vector.quantize_mx(
                 out=v_codes[t][:].bitcast(FP8X4),
                 scales=v_scales[t][:],
@@ -108,6 +118,8 @@ def tile_attend_plo_wsum_f_topk_kernel(tc, vT, wT, gn, offs, out_0, out_1, out_2
             nc.scalar.activation(out=y[h][t // 2][:, t % 2, :], in_=acc[:], func=SILU, scale=gains[:, t : t + 1])
 
         def hand_out_pair(h, u):
+            if u == 0:
+                y_grouped[h] = late.tile([P, HALF, PACK], BF16, name=f"y_grouped{h}", align_bytes=64, offset=(2 + h) * POOL_BYTES)
             cols = slice(h * HALF, (h + 1) * HALF)
             nc.sync.dma_start(out=y_rows[:, 2 * u : 2 * u + 2, cols], in_=y[h][u][:])
             nc.vector.tensor_copy(
@@ -125,29 +137,35 @@ def tile_attend_plo_wsum_f_topk_kernel(tc, vT, wT, gn, offs, out_0, out_1, out_2
             nc.sync.dma_start(out=y_words[:, cols], in_=y_codes[h][:].bitcast(I32))
 
         gather_and_turn(0)
-        group_weights(0)
+        group_values(0)
+        gather_and_turn(1)
+        group_values(1)
+        group_weights(nc.vector.tensor_copy, 0, slice(0, HALF))
         quantize_values(0)
         quantize_weights(0)
+        quantize_values(1)
         multiply(0, 0)
-        for t in (1, 2):
-            gather_and_turn(t)
-            quantize_values(t)
-            multiply(t, 0)
-            if t == 1:
-                hand_out_pair(0, 0)
+        multiply(1, 0)
+        gather_and_turn(2)
+        group_values(2)
+        hand_out_pair(0, 0)
         gather_and_turn(3)
-        group_weights(1)
-        quantize_values(3)
+        group_weights(nc.scalar.copy, 1, slice(0, SCALAR_COLS))
+        group_weights(nc.vector.tensor_copy, 1, slice(SCALAR_COLS, HALF))
+        group_values(3)
+        quantize_values(2)
         quantize_weights(1)
-        multiply(3, 0)
+        quantize_values(3)
+        multiply(2, 0)
         multiply(0, 1)
         multiply(1, 1)
-        hand_out_pair(0, 1)
-        quantize_result(0)
         hand_out_pair(1, 0)
         multiply(2, 1)
+        multiply(3, 0)
         multiply(3, 1)
+        hand_out_pair(0, 1)
         hand_out_pair(1, 1)
+        quantize_result(0)
         quantize_result(1)
         for quad in range(4):
             queue = nc.scalar if quad % 2 == 0 else nc.sync

@@ -16,13 +16,26 @@ P = 128
 PACK = 4
 SLOTS = 512
 TOKENS = 2048
+FEATURES = 512
 QUERIES = 512
 HALF = QUERIES // 2
+LINE = 4
+MX_ALIGN = 64
 
 SCALAR_COLS = 96
-POOL_BYTES = 4 * TOKENS
 
-FLOPS = 2 * 512 * 512 * 512
+SHELF_BYTES = 4 * TOKENS
+SHELVES = (
+    "plane0", "plane1", "plane2", "plane3", "w_raw0", "w_raw1", "v_grouped0", "v_grouped1", "v_grouped2",
+    "w_grouped0", "w_grouped1", "v_codes1",
+)
+BESIDE_CODES = 1024
+
+V_CODES_SHELF = ("plane1", "v_codes1", "w_raw1", "w_grouped1")
+V_GROUPED_SHELF = ("v_grouped0", "v_grouped1", "v_grouped2", "w_raw1")
+Y_GROUPED_SHELF = ("plane2", "plane3")
+
+FLOPS = 2 * FEATURES * SLOTS * QUERIES
 
 
 def tile_attend_plo_wsum_f_topk_kernel(tc, vT, wT, gn, offs, out_0, out_1, out_2):
@@ -30,78 +43,90 @@ def tile_attend_plo_wsum_f_topk_kernel(tc, vT, wT, gn, offs, out_0, out_1, out_2
     v_rows = vT.rearrange("(p t) n -> p t n", t=PACK)
     w_rows = wT[0].rearrange("(p j) q -> p j q", j=PACK)
     y_rows = out_0.rearrange("(p t) q -> p t q", t=PACK)
-    y_words = out_1[0].rearrange("p q u -> p (q u)").bitcast(I32)
+    y_words = out_1[0].rearrange("p q t -> p (q t)").bitcast(I32)
     y_scale_rows = out_2[0].bitcast(I32)
+    halves = (slice(0, HALF), slice(HALF, QUERIES))
 
     with ExitStack() as ctx:
         keep = ctx.enter_context(tc.tile_pool(name="keep", bufs=1))
-        late = ctx.enter_context(tc.tile_pool(name="late", bufs=1))
+        shelved = ctx.enter_context(tc.tile_pool(name="shelved", bufs=1))
         turn = ctx.enter_context(tc.psum_pool(name="turn", bufs=2))
         sums = ctx.enter_context(tc.psum_pool(name="sums", bufs=6))
 
+        def on_shelf(shape, dtype, name, shelf, skip=0):
+            offset = SHELVES.index(shelf) * SHELF_BYTES + skip
+            return shelved.tile(shape, dtype, name=name, align_bytes=MX_ALIGN, offset=offset)
+
         offsets = keep.tile([P, SLOTS // 16], U16, name="offsets")
         gains = keep.tile([P, PACK], F32, name="gains")
-        pools = [late.tile([P, TOKENS], F32, name=f"pool{t}", align_bytes=64, offset=t * POOL_BYTES) for t in range(PACK)]
-        w_raw = [late.tile([P, PACK, HALF], F32, name=f"w_raw{h}", align_bytes=64, offset=(PACK + h) * POOL_BYTES) for h in range(2)]
+        planes = [on_shelf([P, TOKENS], F32, f"plane{t}", f"plane{t}") for t in range(PACK)]
+        w_raw = [on_shelf([P, PACK, HALF], F32, f"w_raw{h}", f"w_raw{h}") for h in range(2)]
 
-        nc.sync.dma_start(out=pools[0][:], in_=v_rows[:, 0, :])
+        nc.sync.dma_start(out=planes[0][:], in_=v_rows[:, 0, :])
         nc.sync.dma_start(offsets[:], offs)
         nc.sync.dma_start(out=gains[:], in_=gn[0].rearrange("(p t) o -> p (t o)", t=PACK))
-        nc.sync.dma_start(out=pools[1][:], in_=v_rows[:, 1, :])
-        nc.sync.dma_start(out=w_raw[0][:], in_=w_rows[:, :, 0:HALF])
-        nc.sync.dma_start(out=pools[2][:], in_=v_rows[:, 2, :])
-        nc.sync.dma_start(out=pools[3][:], in_=v_rows[:, 3, :])
-        nc.sync.dma_start(out=w_raw[1][:], in_=w_rows[:, :, HALF:QUERIES])
+        nc.sync.dma_start(out=planes[1][:], in_=v_rows[:, 1, :])
+        nc.sync.dma_start(out=w_raw[0][:], in_=w_rows[:, :, halves[0]])
+        nc.sync.dma_start(out=planes[2][:], in_=v_rows[:, 2, :])
+        nc.sync.dma_start(out=planes[3][:], in_=v_rows[:, 3, :])
+        nc.sync.dma_start(out=w_raw[1][:], in_=w_rows[:, :, halves[1]])
 
         identity = keep.tile([P, P], F32, name="identity")
         make_identity(nc, identity[:])
 
-        v_codes = {}
-        v_scales = [keep.tile([P, P], U8, name=f"v_scales{t}", align_bytes=64) for t in range(PACK)]
-        w_codes = [keep.tile([P, HALF], U32, name=f"w_codes{h}", align_bytes=64) for h in range(2)]
-        w_scales = [keep.tile([P, HALF], U8, name=f"w_scales{h}", align_bytes=64) for h in range(2)]
-        w_grouped = [late.tile([P, HALF, PACK], BF16, name=f"w_grouped{h}", align_bytes=64, offset=(9 + h) * POOL_BYTES) for h in range(2)]
-        v_grouped = {}
-        turned = {}
-        y = [[keep.tile([P, 2, HALF], F32, name=f"y{h}{u}") for u in range(2)] for h in range(2)]
-        y_grouped = {}
-        y_codes = [keep.tile([P, HALF], U32, name=f"y_codes{h}", align_bytes=64) for h in range(2)]
-        y_scales = keep.tile([P, QUERIES], U8, name="y_scales", align_bytes=64)
+        v_scales = [keep.tile([P, P], U8, name=f"v_scales{t}", align_bytes=MX_ALIGN) for t in range(PACK)]
+        w_codes = [keep.tile([P, HALF], U32, name=f"w_codes{h}", align_bytes=MX_ALIGN) for h in range(2)]
+        w_scales = [keep.tile([P, HALF], U8, name=f"w_scales{h}", align_bytes=MX_ALIGN) for h in range(2)]
+        w_grouped = [on_shelf([P, HALF, PACK], BF16, f"w_grouped{h}", f"w_grouped{h}") for h in range(2)]
+        y_early = keep.tile([P, 2, HALF], F32, name="y_early")
+        late_rows = ((2, 0), (0, 1), (1, 1), (2, 1), (3, 0), (3, 1))
+        y_late = keep.tile([P, len(late_rows), HALF], F32, name="y_late")
+        y = {(t, 0): y_early[:, t, :] for t in range(2)}
+        for row, plane_and_half in enumerate(late_rows):
+            y[plane_and_half] = y_late[:, row, :]
+
+        def late_pair(h, u):
+            first, second = late_rows.index((2 * u, h)), late_rows.index((2 * u + 1, h))
+            return y_late[:, first : second + 1 : second - first, :]
+
+        y_codes = [keep.tile([P, HALF], U32, name=f"y_codes{h}", align_bytes=MX_ALIGN) for h in range(2)]
+        y_scales = keep.tile([P, QUERIES], U8, name="y_scales", align_bytes=MX_ALIGN)
+        turned, v_grouped, v_codes, y_grouped = {}, {}, {}, {}
 
         def group_weights(copy, h, cols):
             copy(
-                out=w_grouped[h][:, cols, :].rearrange("p (c i) j -> p c j i", i=4),
-                in_=w_raw[h][:, :, cols].rearrange("p j (c i) -> p c j i", i=4),
+                out=w_grouped[h][:, cols, :].rearrange("s (c i) j -> s c j i", i=LINE),
+                in_=w_raw[h][:, :, cols].rearrange("s j (c i) -> s c j i", i=LINE),
             )
 
         def quantize_weights(h):
             nc.vector.quantize_mx(
                 out=w_codes[h][:].bitcast(FP8X4),
                 scales=w_scales[h][:],
-                in_=w_grouped[h][:].rearrange("p q j -> p (q j)"),
+                in_=w_grouped[h][:].rearrange("s q j -> s (q j)"),
             )
 
         def gather_and_turn(t):
-            picked = keep.tile([P, SLOTS], BF16, name=f"picked{t}", align_bytes=64)
-            nc.vector.tensor_copy(picked[:], pools[t][:].indirect(offsets[:]))
-            pairs = picked[:].bitcast(F32)
+            picked = keep.tile([P, SLOTS], BF16, name=f"picked{t}", align_bytes=MX_ALIGN)
+            nc.vector.tensor_copy(picked[:], planes[t][:].indirect(offsets[:]))
+            slot_pairs = picked[:].bitcast(F32)
             turned[t] = turn.tile([P, 2, P], F32, name="turned")
             for u in range(2):
-                nc.tensor.transpose(turned[t][:, u, :], pairs[:, u : SLOTS // 2 : 2], identity[:])
+                nc.tensor.transpose(turned[t][:, u, :], slot_pairs[:, u : SLOTS // 2 : 2], identity[:])
 
         def group_values(t):
-            v_grouped[t] = late.tile([P, P, PACK], BF16, name=f"v_grouped{t}", align_bytes=64, offset=(6, 7, 8, 5)[t] * POOL_BYTES + 1024)
+            v_grouped[t] = on_shelf([P, P, PACK], BF16, f"v_grouped{t}", V_GROUPED_SHELF[t], skip=BESIDE_CODES)
             nc.scalar.copy(
-                out=v_grouped[t][:].rearrange("s m j -> s (m j)").bitcast(F32).rearrange("s (m u) -> s m u", u=2),
-                in_=turned[t][:].rearrange("s u m -> s m u"),
+                out=v_grouped[t][:].rearrange("s p j -> s (p j)").bitcast(F32).rearrange("s (p u) -> s p u", u=2),
+                in_=turned[t][:].rearrange("s u p -> s p u"),
             )
 
         def quantize_values(t):
-            v_codes[t] = late.tile([P, P], U32, name=f"v_codes{t}", align_bytes=64, offset=(1, 11, 5, 10)[t] * POOL_BYTES)
+            v_codes[t] = on_shelf([P, P], U32, f"v_codes{t}", V_CODES_SHELF[t])
             nc.vector.quantize_mx(
                 out=v_codes[t][:].bitcast(FP8X4),
                 scales=v_scales[t][:],
-                in_=v_grouped[t][:].rearrange("s m j -> s (m j)"),
+                in_=v_grouped[t][:].rearrange("s p j -> s (p j)"),
             )
 
         def multiply(t, h):
@@ -115,31 +140,27 @@ def tile_attend_plo_wsum_f_topk_kernel(tc, vT, wT, gn, offs, out_0, out_1, out_2
                 start=True,
                 stop=True,
             )
-            nc.scalar.activation(out=y[h][t // 2][:, t % 2, :], in_=acc[:], func=SILU, scale=gains[:, t : t + 1])
+            nc.scalar.activation(out=y[t, h], in_=acc[:], func=SILU, scale=gains[:, t : t + 1])
 
-        def hand_out_pair(h, u):
+        def group_results(h, u, pair):
             if u == 0:
-                y_grouped[h] = late.tile([P, HALF, PACK], BF16, name=f"y_grouped{h}", align_bytes=64, offset=(2 + h) * POOL_BYTES)
-            cols = slice(h * HALF, (h + 1) * HALF)
-            nc.sync.dma_start(out=y_rows[:, 2 * u : 2 * u + 2, cols], in_=y[h][u][:])
+                y_grouped[h] = on_shelf([P, HALF, PACK], BF16, f"y_grouped{h}", Y_GROUPED_SHELF[h])
             nc.vector.tensor_copy(
-                out=y_grouped[h][:, :, 2 * u : 2 * u + 2].rearrange("p (c i) e -> p c e i", i=4),
-                in_=y[h][u][:].rearrange("p e (c i) -> p c e i", i=4),
+                out=y_grouped[h][:, :, 2 * u : 2 * u + 2].rearrange("p (c i) e -> p c e i", i=LINE),
+                in_=pair.rearrange("p e (c i) -> p c e i", i=LINE),
             )
 
-        def quantize_result(h):
-            cols = slice(h * HALF, (h + 1) * HALF)
+        def quantize_results(h):
             nc.vector.quantize_mx(
                 out=y_codes[h][:].bitcast(FP8X4),
-                scales=y_scales[:, cols],
+                scales=y_scales[:, halves[h]],
                 in_=y_grouped[h][:].rearrange("p q t -> p (q t)"),
             )
-            nc.sync.dma_start(out=y_words[:, cols], in_=y_codes[h][:].bitcast(I32))
+            nc.sync.dma_start(out=y_words[:, halves[h]], in_=y_codes[h][:].bitcast(I32))
 
-        gather_and_turn(0)
-        group_values(0)
-        gather_and_turn(1)
-        group_values(1)
+        for t in (0, 1):
+            gather_and_turn(t)
+            group_values(t)
         group_weights(nc.vector.tensor_copy, 0, slice(0, HALF))
         quantize_values(0)
         quantize_weights(0)
@@ -148,7 +169,9 @@ def tile_attend_plo_wsum_f_topk_kernel(tc, vT, wT, gn, offs, out_0, out_1, out_2
         multiply(1, 0)
         gather_and_turn(2)
         group_values(2)
-        hand_out_pair(0, 0)
+        nc.sync.dma_start(out=y_rows[:, 0:2, halves[0]], in_=y_early[:])
+        group_results(0, 0, y_early[:])
+
         gather_and_turn(3)
         group_weights(nc.scalar.copy, 1, slice(0, SCALAR_COLS))
         group_weights(nc.vector.tensor_copy, 1, slice(SCALAR_COLS, HALF))
@@ -156,18 +179,23 @@ def tile_attend_plo_wsum_f_topk_kernel(tc, vT, wT, gn, offs, out_0, out_1, out_2
         quantize_values(2)
         quantize_weights(1)
         quantize_values(3)
+
         multiply(2, 0)
+        nc.sync.dma_start(out=y_rows[:, 2, halves[0]], in_=y[2, 0])
         multiply(0, 1)
         multiply(1, 1)
-        hand_out_pair(1, 0)
+        group_results(1, 0, late_pair(1, 0))
         multiply(2, 1)
+        nc.sync.dma_start(out=y_rows[:, 0:3, halves[1]], in_=y_late[:, 1:4, :])
         multiply(3, 0)
         multiply(3, 1)
-        hand_out_pair(0, 1)
-        hand_out_pair(1, 1)
-        quantize_result(0)
-        quantize_result(1)
-        for quad in range(4):
+        nc.sync.dma_start(out=y_rows[:, 3, :], in_=y_late[:, 4:6, :].rearrange("p h q -> p (h q)"))
+        group_results(0, 1, late_pair(0, 1))
+        group_results(1, 1, late_pair(1, 1))
+        quantize_results(0)
+        quantize_results(1)
+
+        for quad in range(P // 32):
             queue = nc.scalar if quad % 2 == 0 else nc.sync
             queue.dma_start(
                 out=y_scale_rows[4 * quad : 4 * quad + 4, :],

@@ -14,26 +14,23 @@ SILU = mybir.ActivationFunctionType.Silu
 
 P = 128
 PACK = 4
+LAST = PACK - 1
 SLOTS = 512
 TOKENS = 2048
 FEATURES = 512
 QUERIES = 512
 HALF = QUERIES // 2
+QUARTER = QUERIES // 4
 LINE = 4
 MX_ALIGN = 64
 
-SCALAR_COLS = 96
-
+SCALAR_COLS = (96, 64)
+SCALAR_RESULT_COLS = 64
 SHELF_BYTES = 4 * TOKENS
-SHELVES = (
-    "plane0", "plane1", "plane2", "plane3", "w_raw0", "w_raw1", "v_grouped0", "v_grouped1", "v_grouped2",
-    "w_grouped0", "w_grouped1", "v_codes1",
-)
+SHELVES = ("plane0", "plane1", "plane2", "plane3", "w_raw0", "w_raw1", "v_grouped0", "v_grouped1", "v_grouped2")
 BESIDE_CODES = 1024
-
-V_CODES_SHELF = ("plane1", "v_codes1", "w_raw1", "w_grouped1")
-V_GROUPED_SHELF = ("v_grouped0", "v_grouped1", "v_grouped2", "w_raw1")
-Y_GROUPED_SHELF = ("plane2", "plane3")
+V_CODES_SHELF = ("plane1", "plane2", "w_raw0", "w_raw1")
+V_GROUPED_SHELF = ("v_grouped0", "v_grouped1", "v_grouped2", "w_raw0")
 
 FLOPS = 2 * FEATURES * SLOTS * QUERIES
 
@@ -59,39 +56,32 @@ def tile_attend_plo_wsum_f_topk_kernel(tc, vT, wT, gn, offs, out_0, out_1, out_2
 
         offsets = keep.tile([P, SLOTS // 16], U16, name="offsets")
         gains = keep.tile([P, PACK], F32, name="gains")
-        planes = [on_shelf([P, TOKENS], F32, f"plane{t}", f"plane{t}") for t in range(PACK)]
         w_raw = [on_shelf([P, PACK, HALF], F32, f"w_raw{h}", f"w_raw{h}") for h in range(2)]
+        planes = [on_shelf([P, TOKENS], F32, f"plane{t}", f"plane{t}") for t in range(PACK)]
 
         nc.sync.dma_start(out=planes[0][:], in_=v_rows[:, 0, :])
         nc.sync.dma_start(offsets[:], offs)
         nc.sync.dma_start(out=gains[:], in_=gn[0].rearrange("(p t) o -> p (t o)", t=PACK))
         nc.sync.dma_start(out=planes[1][:], in_=v_rows[:, 1, :])
-        nc.sync.dma_start(out=w_raw[0][:], in_=w_rows[:, :, halves[0]])
         nc.sync.dma_start(out=planes[2][:], in_=v_rows[:, 2, :])
-        nc.sync.dma_start(out=planes[3][:], in_=v_rows[:, 3, :])
+        nc.sync.dma_start(out=planes[LAST][:], in_=v_rows[:, LAST, :])
+        nc.sync.dma_start(out=w_raw[0][:], in_=w_rows[:, :, halves[0]])
         nc.sync.dma_start(out=w_raw[1][:], in_=w_rows[:, :, halves[1]])
 
         identity = keep.tile([P, P], F32, name="identity")
         make_identity(nc, identity[:])
+        table_warm_up = keep.tile([P, 1], F32, name="table_warm_up")
+        nc.scalar.activation(out=table_warm_up[:], in_=identity[:, 0:1], func=SILU)
 
         v_scales = [keep.tile([P, P], U8, name=f"v_scales{t}", align_bytes=MX_ALIGN) for t in range(PACK)]
+        w_grouped = [keep.tile([P, HALF, PACK], BF16, name=f"w_grouped{h}", align_bytes=MX_ALIGN) for h in range(2)]
         w_codes = [keep.tile([P, HALF], U32, name=f"w_codes{h}", align_bytes=MX_ALIGN) for h in range(2)]
         w_scales = [keep.tile([P, HALF], U8, name=f"w_scales{h}", align_bytes=MX_ALIGN) for h in range(2)]
-        w_grouped = [on_shelf([P, HALF, PACK], BF16, f"w_grouped{h}", f"w_grouped{h}") for h in range(2)]
-        y_early = keep.tile([P, 2, HALF], F32, name="y_early")
-        late_rows = ((2, 0), (0, 1), (1, 1), (2, 1), (3, 0), (3, 1))
-        y_late = keep.tile([P, len(late_rows), HALF], F32, name="y_late")
-        y = {(t, 0): y_early[:, t, :] for t in range(2)}
-        for row, plane_and_half in enumerate(late_rows):
-            y[plane_and_half] = y_late[:, row, :]
-
-        def late_pair(h, u):
-            first, second = late_rows.index((2 * u, h)), late_rows.index((2 * u + 1, h))
-            return y_late[:, first : second + 1 : second - first, :]
-
+        y = [keep.tile([P, PACK, HALF], F32, name=f"y{h}") for h in range(2)]
         y_codes = [keep.tile([P, HALF], U32, name=f"y_codes{h}", align_bytes=MX_ALIGN) for h in range(2)]
         y_scales = keep.tile([P, QUERIES], U8, name="y_scales", align_bytes=MX_ALIGN)
-        turned, v_grouped, v_codes, y_grouped = {}, {}, {}, {}
+        y_grouped = [keep.tile([P, HALF, PACK], BF16, name=f"y_grouped{h}", align_bytes=MX_ALIGN) for h in range(2)]
+        picked, turned, v_grouped, v_codes = {}, {}, {}, {}
 
         def group_weights(copy, h, cols):
             copy(
@@ -107,9 +97,9 @@ def tile_attend_plo_wsum_f_topk_kernel(tc, vT, wT, gn, offs, out_0, out_1, out_2
             )
 
         def gather_and_turn(t):
-            picked = keep.tile([P, SLOTS], BF16, name=f"picked{t}", align_bytes=MX_ALIGN)
-            nc.vector.tensor_copy(picked[:], planes[t][:].indirect(offsets[:]))
-            slot_pairs = picked[:].bitcast(F32)
+            picked[t] = keep.tile([P, SLOTS], BF16, name=f"picked{t}", align_bytes=MX_ALIGN)
+            nc.vector.tensor_copy(picked[t][:], planes[t][:].indirect(offsets[:]))
+            slot_pairs = picked[t][:].bitcast(F32)
             turned[t] = turn.tile([P, 2, P], F32, name="turned")
             for u in range(2):
                 nc.tensor.transpose(turned[t][:, u, :], slot_pairs[:, u : SLOTS // 2 : 2], identity[:])
@@ -140,14 +130,15 @@ def tile_attend_plo_wsum_f_topk_kernel(tc, vT, wT, gn, offs, out_0, out_1, out_2
                 start=True,
                 stop=True,
             )
-            nc.scalar.activation(out=y[t, h], in_=acc[:], func=SILU, scale=gains[:, t : t + 1])
+            nc.scalar.activation(out=y[h][:, t, :], in_=acc[:], func=SILU, scale=gains[:, t : t + 1])
 
-        def group_results(h, u, pair):
-            if u == 0:
-                y_grouped[h] = on_shelf([P, HALF, PACK], BF16, f"y_grouped{h}", Y_GROUPED_SHELF[h])
-            nc.vector.tensor_copy(
-                out=y_grouped[h][:, :, 2 * u : 2 * u + 2].rearrange("p (c i) e -> p c e i", i=LINE),
-                in_=pair.rearrange("p e (c i) -> p c e i", i=LINE),
+        def store_pair(h, u):
+            nc.sync.dma_start(out=y_rows[:, 2 * u : 2 * u + 2, halves[h]], in_=y[h][:, 2 * u : 2 * u + 2, :])
+
+        def group_results(copy, h, cols):
+            copy(
+                out=y_grouped[h][:, cols, :].rearrange("p (c i) t -> p c t i", i=LINE),
+                in_=y[h][:, :, cols].rearrange("p t (c i) -> p c t i", i=LINE),
             )
 
         def quantize_results(h):
@@ -158,42 +149,35 @@ def tile_attend_plo_wsum_f_topk_kernel(tc, vT, wT, gn, offs, out_0, out_1, out_2
             )
             nc.sync.dma_start(out=y_words[:, halves[h]], in_=y_codes[h][:].bitcast(I32))
 
-        for t in (0, 1):
+        for t in range(2):
             gather_and_turn(t)
             group_values(t)
-        group_weights(nc.vector.tensor_copy, 0, slice(0, HALF))
         quantize_values(0)
-        quantize_weights(0)
-        quantize_values(1)
-        multiply(0, 0)
-        multiply(1, 0)
         gather_and_turn(2)
         group_values(2)
-        nc.sync.dma_start(out=y_rows[:, 0:2, halves[0]], in_=y_early[:])
-        group_results(0, 0, y_early[:])
-
-        gather_and_turn(3)
-        group_weights(nc.scalar.copy, 1, slice(0, SCALAR_COLS))
-        group_weights(nc.vector.tensor_copy, 1, slice(SCALAR_COLS, HALF))
-        group_values(3)
+        quantize_values(1)
+        gather_and_turn(LAST)
+        group_weights(nc.scalar.copy, 0, slice(0, SCALAR_COLS[0]))
+        group_weights(nc.vector.tensor_copy, 0, slice(SCALAR_COLS[0], HALF))
+        group_values(LAST)
         quantize_values(2)
+        quantize_weights(0)
+        group_weights(nc.scalar.copy, 1, slice(0, SCALAR_COLS[1]))
+        group_weights(nc.vector.tensor_copy, 1, slice(SCALAR_COLS[1], HALF))
+        quantize_values(LAST)
         quantize_weights(1)
-        quantize_values(3)
-
-        multiply(2, 0)
-        nc.sync.dma_start(out=y_rows[:, 2, halves[0]], in_=y[2, 0])
-        multiply(0, 1)
-        multiply(1, 1)
-        group_results(1, 0, late_pair(1, 0))
-        multiply(2, 1)
-        nc.sync.dma_start(out=y_rows[:, 0:3, halves[1]], in_=y_late[:, 1:4, :])
-        multiply(3, 0)
-        multiply(3, 1)
-        nc.sync.dma_start(out=y_rows[:, 3, :], in_=y_late[:, 4:6, :].rearrange("p h q -> p (h q)"))
-        group_results(0, 1, late_pair(0, 1))
-        group_results(1, 1, late_pair(1, 1))
-        quantize_results(0)
-        quantize_results(1)
+        for h in range(2):
+            for t in range(PACK):
+                multiply(t, h)
+            for u in range(2):
+                store_pair(h, u)
+            if h == 0:
+                group_results(nc.vector.tensor_copy, h, slice(0, HALF))
+            else:
+                group_results(nc.vector.tensor_copy, h, slice(SCALAR_RESULT_COLS, HALF))
+                group_results(nc.scalar.copy, h, slice(0, SCALAR_RESULT_COLS))
+        for h in range(2):
+            quantize_results(h)
 
         for quad in range(P // 32):
             queue = nc.scalar if quad % 2 == 0 else nc.sync

@@ -24,13 +24,18 @@ QUARTER = QUERIES // 4
 LINE = 4
 MX_ALIGN = 64
 
+PIECES = ((0, 256), (256, 512))
+SHELF_BYTES = 4 * TOKENS
+SHELVES = (
+    "plane0", "plane1", "plane2", "plane3", "w_raw0", "w_raw1", "w_raw2", "w_grouped0", "w_grouped1",
+    "v_grouped0", "v_grouped1", "v_grouped2",
+)
+KIB = 1024
+V_CODES_AT = (("plane1", 0), ("plane2", 0), ("w_raw0", 0), ("w_raw1", 0))
+V_GROUPED_AT = (("v_grouped0", 0), ("v_grouped1", 0), ("v_grouped2", 0), ("w_raw0", KIB))
+W_GROUPED_AT = (("w_grouped0", 0), ("w_grouped1", 0))
 SCALAR_COLS = (96, 64)
 SCALAR_RESULT_COLS = 64
-SHELF_BYTES = 4 * TOKENS
-SHELVES = ("plane0", "plane1", "plane2", "plane3", "w_raw0", "w_raw1", "v_grouped0", "v_grouped1", "v_grouped2")
-BESIDE_CODES = 1024
-V_CODES_SHELF = ("plane1", "plane2", "w_raw0", "w_raw1")
-V_GROUPED_SHELF = ("v_grouped0", "v_grouped1", "v_grouped2", "w_raw0")
 
 FLOPS = 2 * FEATURES * SLOTS * QUERIES
 
@@ -42,7 +47,8 @@ def tile_attend_plo_wsum_f_topk_kernel(tc, vT, wT, gn, offs, out_0, out_1, out_2
     y_rows = out_0.rearrange("(p t) q -> p t q", t=PACK)
     y_words = out_1[0].rearrange("p q t -> p (q t)").bitcast(I32)
     y_scale_rows = out_2[0].bitcast(I32)
-    halves = (slice(0, HALF), slice(HALF, QUERIES))
+    pieces = [slice(first, end) for first, end in PIECES]
+    widths = [end - first for first, end in PIECES]
 
     with ExitStack() as ctx:
         keep = ctx.enter_context(tc.tile_pool(name="keep", bufs=1))
@@ -56,17 +62,16 @@ def tile_attend_plo_wsum_f_topk_kernel(tc, vT, wT, gn, offs, out_0, out_1, out_2
 
         offsets = keep.tile([P, SLOTS // 16], U16, name="offsets")
         gains = keep.tile([P, PACK], F32, name="gains")
-        w_raw = [on_shelf([P, PACK, HALF], F32, f"w_raw{h}", f"w_raw{h}") for h in range(2)]
+        w_raw = [on_shelf([P, PACK, n], F32, f"w_raw{k}", f"w_raw{k}") for k, n in enumerate(widths)]
         planes = [on_shelf([P, TOKENS], F32, f"plane{t}", f"plane{t}") for t in range(PACK)]
 
         nc.sync.dma_start(out=planes[0][:], in_=v_rows[:, 0, :])
         nc.sync.dma_start(offsets[:], offs)
-        nc.sync.dma_start(out=gains[:], in_=gn[0].rearrange("(p t) o -> p (t o)", t=PACK))
-        nc.sync.dma_start(out=planes[1][:], in_=v_rows[:, 1, :])
-        nc.sync.dma_start(out=planes[2][:], in_=v_rows[:, 2, :])
-        nc.sync.dma_start(out=planes[LAST][:], in_=v_rows[:, LAST, :])
-        nc.sync.dma_start(out=w_raw[0][:], in_=w_rows[:, :, halves[0]])
-        nc.sync.dma_start(out=w_raw[1][:], in_=w_rows[:, :, halves[1]])
+        nc.scalar.dma_start(out=gains[:], in_=gn[0].rearrange("(p t) o -> p (t o)", t=PACK))
+        for t in range(1, PACK):
+            nc.sync.dma_start(out=planes[t][:], in_=v_rows[:, t, :])
+        for k, cols in enumerate(pieces):
+            nc.sync.dma_start(out=w_raw[k][:], in_=w_rows[:, :, cols])
 
         identity = keep.tile([P, P], F32, name="identity")
         make_identity(nc, identity[:])
@@ -74,26 +79,34 @@ def tile_attend_plo_wsum_f_topk_kernel(tc, vT, wT, gn, offs, out_0, out_1, out_2
         nc.scalar.activation(out=table_warm_up[:], in_=identity[:, 0:1], func=SILU)
 
         v_scales = [keep.tile([P, P], U8, name=f"v_scales{t}", align_bytes=MX_ALIGN) for t in range(PACK)]
-        w_grouped = [keep.tile([P, HALF, PACK], BF16, name=f"w_grouped{h}", align_bytes=MX_ALIGN) for h in range(2)]
-        w_codes = [keep.tile([P, HALF], U32, name=f"w_codes{h}", align_bytes=MX_ALIGN) for h in range(2)]
-        w_scales = [keep.tile([P, HALF], U8, name=f"w_scales{h}", align_bytes=MX_ALIGN) for h in range(2)]
-        y = [keep.tile([P, PACK, HALF], F32, name=f"y{h}") for h in range(2)]
-        y_codes = [keep.tile([P, HALF], U32, name=f"y_codes{h}", align_bytes=MX_ALIGN) for h in range(2)]
+        w_codes = [keep.tile([P, n], U32, name=f"w_codes{k}", align_bytes=MX_ALIGN) for k, n in enumerate(widths)]
+        w_scales = [keep.tile([P, n], U8, name=f"w_scales{k}", align_bytes=MX_ALIGN) for k, n in enumerate(widths)]
+        y = [keep.tile([P, PACK, n], F32, name=f"y{k}") for k, n in enumerate(widths)]
+        y_grouped = [
+            keep.tile([P, n, PACK], BF16, name=f"y_grouped{k}", align_bytes=MX_ALIGN) for k, n in enumerate(widths)
+        ]
+        y_codes = [keep.tile([P, n], U32, name=f"y_codes{k}", align_bytes=MX_ALIGN) for k, n in enumerate(widths)]
         y_scales = keep.tile([P, QUERIES], U8, name="y_scales", align_bytes=MX_ALIGN)
-        y_grouped = [keep.tile([P, HALF, PACK], BF16, name=f"y_grouped{h}", align_bytes=MX_ALIGN) for h in range(2)]
-        picked, turned, v_grouped, v_codes = {}, {}, {}, {}
+        picked, turned, v_grouped, v_codes, w_grouped = {}, {}, {}, {}, {}
 
-        def group_weights(copy, h, cols):
+        def group(copy, grouped, rows, cols):
             copy(
-                out=w_grouped[h][:, cols, :].rearrange("s (c i) j -> s c j i", i=LINE),
-                in_=w_raw[h][:, :, cols].rearrange("s j (c i) -> s c j i", i=LINE),
+                out=grouped[:, cols, :].rearrange("p (c i) j -> p c j i", i=LINE),
+                in_=rows[:, :, cols].rearrange("p j (c i) -> p c j i", i=LINE),
             )
 
-        def quantize_weights(h):
+        def group_weights(k, scalar_cols):
+            w_grouped[k] = on_shelf([P, widths[k], PACK], BF16, f"w_grouped{k}", *W_GROUPED_AT[k])
+            if scalar_cols > 0:
+                group(nc.scalar.copy, w_grouped[k], w_raw[k], slice(0, scalar_cols))
+            if scalar_cols < widths[k]:
+                group(nc.vector.tensor_copy, w_grouped[k], w_raw[k], slice(scalar_cols, widths[k]))
+
+        def quantize_weights(k):
             nc.vector.quantize_mx(
-                out=w_codes[h][:].bitcast(FP8X4),
-                scales=w_scales[h][:],
-                in_=w_grouped[h][:].rearrange("s q j -> s (q j)"),
+                out=w_codes[k][:].bitcast(FP8X4),
+                scales=w_scales[k][:],
+                in_=w_grouped[k][:].rearrange("s q j -> s (q j)"),
             )
 
         def gather_and_turn(t):
@@ -105,50 +118,48 @@ def tile_attend_plo_wsum_f_topk_kernel(tc, vT, wT, gn, offs, out_0, out_1, out_2
                 nc.tensor.transpose(turned[t][:, u, :], slot_pairs[:, u : SLOTS // 2 : 2], identity[:])
 
         def group_values(t):
-            v_grouped[t] = on_shelf([P, P, PACK], BF16, f"v_grouped{t}", V_GROUPED_SHELF[t], skip=BESIDE_CODES)
+            v_grouped[t] = on_shelf([P, P, PACK], BF16, f"v_grouped{t}", *V_GROUPED_AT[t])
             nc.scalar.copy(
                 out=v_grouped[t][:].rearrange("s p j -> s (p j)").bitcast(F32).rearrange("s (p u) -> s p u", u=2),
                 in_=turned[t][:].rearrange("s u p -> s p u"),
             )
 
         def quantize_values(t):
-            v_codes[t] = on_shelf([P, P], U32, f"v_codes{t}", V_CODES_SHELF[t])
+            v_codes[t] = on_shelf([P, P], U32, f"v_codes{t}", *V_CODES_AT[t])
             nc.vector.quantize_mx(
                 out=v_codes[t][:].bitcast(FP8X4),
                 scales=v_scales[t][:],
                 in_=v_grouped[t][:].rearrange("s p j -> s (p j)"),
             )
 
-        def multiply(t, h):
-            acc = sums.tile([P, HALF], F32, name="acc")
+        def multiply(t, k, cols):
+            acc = sums.tile([P, cols.stop - cols.start], F32, name="acc")
             nc.tensor.matmul_mx(
                 out=acc[:],
                 lhsT=v_codes[t][:].bitcast(FP8X4),
                 lhsT_scale=v_scales[t][:],
-                rhs=w_codes[h][:].bitcast(FP8X4),
-                rhs_scale=w_scales[h][:],
+                rhs=w_codes[k][:, cols].bitcast(FP8X4),
+                rhs_scale=w_scales[k][:, cols],
                 start=True,
                 stop=True,
             )
-            nc.scalar.activation(out=y[h][:, t, :], in_=acc[:], func=SILU, scale=gains[:, t : t + 1])
+            nc.scalar.activation(out=y[k][:, t, cols], in_=acc[:], func=SILU, scale=gains[:, t : t + 1])
 
-        def store_pair(h, u):
-            nc.sync.dma_start(out=y_rows[:, 2 * u : 2 * u + 2, halves[h]], in_=y[h][:, 2 * u : 2 * u + 2, :])
+        def store_results(k, first, end):
+            nc.sync.dma_start(out=y_rows[:, first:end, pieces[k]], in_=y[k][:, first:end, :])
 
-        def group_results(copy, h, cols):
-            copy(
-                out=y_grouped[h][:, cols, :].rearrange("p (c i) t -> p c t i", i=LINE),
-                in_=y[h][:, :, cols].rearrange("p t (c i) -> p c t i", i=LINE),
-            )
-
-        def quantize_results(h):
+        def quantize_results(k, cols):
+            first = pieces[k].start
             nc.vector.quantize_mx(
-                out=y_codes[h][:].bitcast(FP8X4),
-                scales=y_scales[:, halves[h]],
-                in_=y_grouped[h][:].rearrange("p q t -> p (q t)"),
+                out=y_codes[k][:, cols].bitcast(FP8X4),
+                scales=y_scales[:, first + cols.start : first + cols.stop],
+                in_=y_grouped[k][:, cols, :].rearrange("p q t -> p (q t)"),
             )
-            nc.sync.dma_start(out=y_words[:, halves[h]], in_=y_codes[h][:].bitcast(I32))
 
+        def store_codes(k):
+            nc.sync.dma_start(out=y_words[:, pieces[k]], in_=y_codes[k][:].bitcast(I32))
+
+        whole, left, right = slice(0, HALF), slice(0, QUARTER), slice(QUARTER, HALF)
         for t in range(2):
             gather_and_turn(t)
             group_values(t)
@@ -157,27 +168,32 @@ def tile_attend_plo_wsum_f_topk_kernel(tc, vT, wT, gn, offs, out_0, out_1, out_2
         group_values(2)
         quantize_values(1)
         gather_and_turn(LAST)
-        group_weights(nc.scalar.copy, 0, slice(0, SCALAR_COLS[0]))
-        group_weights(nc.vector.tensor_copy, 0, slice(SCALAR_COLS[0], HALF))
+        group_weights(0, SCALAR_COLS[0])
         group_values(LAST)
         quantize_values(2)
         quantize_weights(0)
-        group_weights(nc.scalar.copy, 1, slice(0, SCALAR_COLS[1]))
-        group_weights(nc.vector.tensor_copy, 1, slice(SCALAR_COLS[1], HALF))
+        group_weights(1, SCALAR_COLS[1])
         quantize_values(LAST)
         quantize_weights(1)
-        for h in range(2):
-            for t in range(PACK):
-                multiply(t, h)
-            for u in range(2):
-                store_pair(h, u)
-            if h == 0:
-                group_results(nc.vector.tensor_copy, h, slice(0, HALF))
-            else:
-                group_results(nc.vector.tensor_copy, h, slice(SCALAR_RESULT_COLS, HALF))
-                group_results(nc.scalar.copy, h, slice(0, SCALAR_RESULT_COLS))
-        for h in range(2):
-            quantize_results(h)
+        for t in range(PACK):
+            multiply(t, 0, whole)
+        store_results(0, 0, 2)
+        store_results(0, 2, PACK)
+        group(nc.vector.tensor_copy, y_grouped[0], y[0], whole)
+        quantize_results(0, whole)
+        store_codes(0)
+        for t in range(LAST):
+            multiply(t, 1, whole)
+        multiply(LAST, 1, left)
+        multiply(LAST, 1, right)
+        store_results(1, 0, 2)
+        store_results(1, 2, PACK)
+        group(nc.vector.tensor_copy, y_grouped[1], y[1], slice(SCALAR_RESULT_COLS, QUARTER))
+        group(nc.scalar.copy, y_grouped[1], y[1], slice(0, SCALAR_RESULT_COLS))
+        group(nc.vector.tensor_copy, y_grouped[1], y[1], right)
+        quantize_results(1, left)
+        quantize_results(1, right)
+        store_codes(1)
 
         for quad in range(P // 32):
             queue = nc.scalar if quad % 2 == 0 else nc.sync

@@ -67,7 +67,7 @@ def tile_attend_plo_wsum_f_topk_kernel(tc, vT, wT, gn, offs, out_0, out_1, out_2
 
         nc.sync.dma_start(out=planes[0][:], in_=v_rows[:, 0, :])
         nc.sync.dma_start(offsets[:], offs)
-        nc.scalar.dma_start(out=gains[:], in_=gn[0].rearrange("(p t) o -> p (t o)", t=PACK))
+        nc.sync.dma_start(out=gains[:], in_=gn[0].rearrange("(p t) o -> p (t o)", t=PACK))
         for t in range(1, PACK):
             nc.sync.dma_start(out=planes[t][:], in_=v_rows[:, t, :])
         for k, cols in enumerate(pieces):

@@ -24,18 +24,17 @@ QUARTER = QUERIES // 4
 LINE = 4
 MX_ALIGN = 64
 
-PIECES = ((0, 256), (256, 512))
+SCALAR_WEIGHT_COLS = (96, 64)
+SCALAR_RESULT_COLS = 64
+
 SHELF_BYTES = 4 * TOKENS
 SHELVES = (
-    "plane0", "plane1", "plane2", "plane3", "w_raw0", "w_raw1", "w_raw2", "w_grouped0", "w_grouped1",
+    "plane0", "plane1", "plane2", "plane3", "w_raw0", "w_raw1", "w_grouped0", "w_grouped1",
     "v_grouped0", "v_grouped1", "v_grouped2",
 )
-KIB = 1024
-V_CODES_AT = (("plane1", 0), ("plane2", 0), ("w_raw0", 0), ("w_raw1", 0))
-V_GROUPED_AT = (("v_grouped0", 0), ("v_grouped1", 0), ("v_grouped2", 0), ("w_raw0", KIB))
-W_GROUPED_AT = (("w_grouped0", 0), ("w_grouped1", 0))
-SCALAR_COLS = (96, 64)
-SCALAR_RESULT_COLS = 64
+BESIDE_CODES = 1024
+V_CODES_SHELF = ("plane1", "plane2", "w_raw0", "w_raw1")
+V_GROUPED_AT = (("v_grouped0", 0), ("v_grouped1", 0), ("v_grouped2", 0), ("w_raw0", BESIDE_CODES))
 
 FLOPS = 2 * FEATURES * SLOTS * QUERIES
 
@@ -47,8 +46,8 @@ def tile_attend_plo_wsum_f_topk_kernel(tc, vT, wT, gn, offs, out_0, out_1, out_2
     y_rows = out_0.rearrange("(p t) q -> p t q", t=PACK)
     y_words = out_1[0].rearrange("p q t -> p (q t)").bitcast(I32)
     y_scale_rows = out_2[0].bitcast(I32)
-    pieces = [slice(first, end) for first, end in PIECES]
-    widths = [end - first for first, end in PIECES]
+    halves = (slice(0, HALF), slice(HALF, QUERIES))
+    whole, left, right = slice(0, HALF), slice(0, QUARTER), slice(QUARTER, HALF)
 
     with ExitStack() as ctx:
         keep = ctx.enter_context(tc.tile_pool(name="keep", bufs=1))
@@ -62,16 +61,16 @@ def tile_attend_plo_wsum_f_topk_kernel(tc, vT, wT, gn, offs, out_0, out_1, out_2
 
         offsets = keep.tile([P, SLOTS // 16], U16, name="offsets")
         gains = keep.tile([P, PACK], F32, name="gains")
-        w_raw = [on_shelf([P, PACK, n], F32, f"w_raw{k}", f"w_raw{k}") for k, n in enumerate(widths)]
+        w_raw = [on_shelf([P, PACK, HALF], F32, f"w_raw{h}", f"w_raw{h}") for h in range(2)]
         planes = [on_shelf([P, TOKENS], F32, f"plane{t}", f"plane{t}") for t in range(PACK)]
 
         nc.sync.dma_start(out=planes[0][:], in_=v_rows[:, 0, :])
         nc.sync.dma_start(offsets[:], offs)
-        nc.sync.dma_start(out=gains[:], in_=gn[0].rearrange("(p t) o -> p (t o)", t=PACK))
         for t in range(1, PACK):
             nc.sync.dma_start(out=planes[t][:], in_=v_rows[:, t, :])
-        for k, cols in enumerate(pieces):
-            nc.sync.dma_start(out=w_raw[k][:], in_=w_rows[:, :, cols])
+        for h in range(2):
+            nc.sync.dma_start(out=w_raw[h][:], in_=w_rows[:, :, halves[h]])
+        nc.sync.dma_start(out=gains[:], in_=gn[0].rearrange("(p t) o -> p (t o)", t=PACK))
 
         identity = keep.tile([P, P], F32, name="identity")
         make_identity(nc, identity[:])
@@ -79,15 +78,13 @@ def tile_attend_plo_wsum_f_topk_kernel(tc, vT, wT, gn, offs, out_0, out_1, out_2
         nc.scalar.activation(out=table_warm_up[:], in_=identity[:, 0:1], func=SILU)
 
         v_scales = [keep.tile([P, P], U8, name=f"v_scales{t}", align_bytes=MX_ALIGN) for t in range(PACK)]
-        w_codes = [keep.tile([P, n], U32, name=f"w_codes{k}", align_bytes=MX_ALIGN) for k, n in enumerate(widths)]
-        w_scales = [keep.tile([P, n], U8, name=f"w_scales{k}", align_bytes=MX_ALIGN) for k, n in enumerate(widths)]
-        y = [keep.tile([P, PACK, n], F32, name=f"y{k}") for k, n in enumerate(widths)]
-        y_grouped = [
-            keep.tile([P, n, PACK], BF16, name=f"y_grouped{k}", align_bytes=MX_ALIGN) for k, n in enumerate(widths)
-        ]
-        y_codes = [keep.tile([P, n], U32, name=f"y_codes{k}", align_bytes=MX_ALIGN) for k, n in enumerate(widths)]
+        w_codes = [keep.tile([P, HALF], U32, name=f"w_codes{h}", align_bytes=MX_ALIGN) for h in range(2)]
+        w_scales = [keep.tile([P, HALF], U8, name=f"w_scales{h}", align_bytes=MX_ALIGN) for h in range(2)]
+        y = [keep.tile([P, PACK, HALF], F32, name=f"y{h}") for h in range(2)]
+        y_grouped = [keep.tile([P, HALF, PACK], BF16, name=f"y_grouped{h}", align_bytes=MX_ALIGN) for h in range(2)]
+        y_codes = [keep.tile([P, HALF], U32, name=f"y_codes{h}", align_bytes=MX_ALIGN) for h in range(2)]
         y_scales = keep.tile([P, QUERIES], U8, name="y_scales", align_bytes=MX_ALIGN)
-        picked, turned, v_grouped, v_codes, w_grouped = {}, {}, {}, {}, {}
+        turned, v_grouped, v_codes, w_grouped = {}, {}, {}, {}
 
         def group(copy, grouped, rows, cols):
             copy(
@@ -95,24 +92,22 @@ def tile_attend_plo_wsum_f_topk_kernel(tc, vT, wT, gn, offs, out_0, out_1, out_2
                 in_=rows[:, :, cols].rearrange("p j (c i) -> p c j i", i=LINE),
             )
 
-        def group_weights(k, scalar_cols):
-            w_grouped[k] = on_shelf([P, widths[k], PACK], BF16, f"w_grouped{k}", *W_GROUPED_AT[k])
-            if scalar_cols > 0:
-                group(nc.scalar.copy, w_grouped[k], w_raw[k], slice(0, scalar_cols))
-            if scalar_cols < widths[k]:
-                group(nc.vector.tensor_copy, w_grouped[k], w_raw[k], slice(scalar_cols, widths[k]))
+        def group_weights(h):
+            w_grouped[h] = on_shelf([P, HALF, PACK], BF16, f"w_grouped{h}", f"w_grouped{h}")
+            group(nc.scalar.copy, w_grouped[h], w_raw[h], slice(0, SCALAR_WEIGHT_COLS[h]))
+            group(nc.vector.tensor_copy, w_grouped[h], w_raw[h], slice(SCALAR_WEIGHT_COLS[h], HALF))
 
-        def quantize_weights(k):
+        def quantize_weights(h):
             nc.vector.quantize_mx(
-                out=w_codes[k][:].bitcast(FP8X4),
-                scales=w_scales[k][:],
-                in_=w_grouped[k][:].rearrange("s q j -> s (q j)"),
+                out=w_codes[h][:].bitcast(FP8X4),
+                scales=w_scales[h][:],
+                in_=w_grouped[h][:].rearrange("s q j -> s (q j)"),
             )
 
         def gather_and_turn(t):
-            picked[t] = keep.tile([P, SLOTS], BF16, name=f"picked{t}", align_bytes=MX_ALIGN)
-            nc.vector.tensor_copy(picked[t][:], planes[t][:].indirect(offsets[:]))
-            slot_pairs = picked[t][:].bitcast(F32)
+            picked = keep.tile([P, SLOTS], BF16, name=f"picked{t}", align_bytes=MX_ALIGN)
+            nc.vector.tensor_copy(picked[:], planes[t][:].indirect(offsets[:]))
+            slot_pairs = picked[:].bitcast(F32)
             turned[t] = turn.tile([P, 2, P], F32, name="turned")
             for u in range(2):
                 nc.tensor.transpose(turned[t][:, u, :], slot_pairs[:, u : SLOTS // 2 : 2], identity[:])
@@ -125,41 +120,41 @@ def tile_attend_plo_wsum_f_topk_kernel(tc, vT, wT, gn, offs, out_0, out_1, out_2
             )
 
         def quantize_values(t):
-            v_codes[t] = on_shelf([P, P], U32, f"v_codes{t}", *V_CODES_AT[t])
+            v_codes[t] = on_shelf([P, P], U32, f"v_codes{t}", V_CODES_SHELF[t])
             nc.vector.quantize_mx(
                 out=v_codes[t][:].bitcast(FP8X4),
                 scales=v_scales[t][:],
                 in_=v_grouped[t][:].rearrange("s p j -> s (p j)"),
             )
 
-        def multiply(t, k, cols):
+        def multiply(t, h, cols):
             acc = sums.tile([P, cols.stop - cols.start], F32, name="acc")
             nc.tensor.matmul_mx(
                 out=acc[:],
                 lhsT=v_codes[t][:].bitcast(FP8X4),
                 lhsT_scale=v_scales[t][:],
-                rhs=w_codes[k][:, cols].bitcast(FP8X4),
-                rhs_scale=w_scales[k][:, cols],
+                rhs=w_codes[h][:, cols].bitcast(FP8X4),
+                rhs_scale=w_scales[h][:, cols],
                 start=True,
                 stop=True,
             )
-            nc.scalar.activation(out=y[k][:, t, cols], in_=acc[:], func=SILU, scale=gains[:, t : t + 1])
+            nc.scalar.activation(out=y[h][:, t, cols], in_=acc[:], func=SILU, scale=gains[:, t : t + 1])
 
-        def store_results(k, first, end):
-            nc.sync.dma_start(out=y_rows[:, first:end, pieces[k]], in_=y[k][:, first:end, :])
+        def store_results(h):
+            for first in (0, 2):
+                nc.sync.dma_start(out=y_rows[:, first : first + 2, halves[h]], in_=y[h][:, first : first + 2, :])
 
-        def quantize_results(k, cols):
-            first = pieces[k].start
+        def quantize_results(h, cols):
+            first = halves[h].start
             nc.vector.quantize_mx(
-                out=y_codes[k][:, cols].bitcast(FP8X4),
+                out=y_codes[h][:, cols].bitcast(FP8X4),
                 scales=y_scales[:, first + cols.start : first + cols.stop],
-                in_=y_grouped[k][:, cols, :].rearrange("p q t -> p (q t)"),
+                in_=y_grouped[h][:, cols, :].rearrange("p q t -> p (q t)"),
             )
 
-        def store_codes(k):
-            nc.sync.dma_start(out=y_words[:, pieces[k]], in_=y_codes[k][:].bitcast(I32))
+        def store_codes(h):
+            nc.sync.dma_start(out=y_words[:, halves[h]], in_=y_codes[h][:].bitcast(I32))
 
-        whole, left, right = slice(0, HALF), slice(0, QUARTER), slice(QUARTER, HALF)
         for t in range(2):
             gather_and_turn(t)
             group_values(t)
@@ -168,26 +163,29 @@ def tile_attend_plo_wsum_f_topk_kernel(tc, vT, wT, gn, offs, out_0, out_1, out_2
         group_values(2)
         quantize_values(1)
         gather_and_turn(LAST)
-        group_weights(0, SCALAR_COLS[0])
+
+        group_weights(0)
         group_values(LAST)
         quantize_values(2)
         quantize_weights(0)
-        group_weights(1, SCALAR_COLS[1])
+        group_weights(1)
         quantize_values(LAST)
         quantize_weights(1)
-        for t in range(PACK):
+
+        multiply(0, 0, left)
+        multiply(0, 0, right)
+        for t in range(1, PACK):
             multiply(t, 0, whole)
-        store_results(0, 0, 2)
-        store_results(0, 2, PACK)
+        store_results(0)
         group(nc.vector.tensor_copy, y_grouped[0], y[0], whole)
         quantize_results(0, whole)
         store_codes(0)
+
         for t in range(LAST):
             multiply(t, 1, whole)
         multiply(LAST, 1, left)
         multiply(LAST, 1, right)
-        store_results(1, 0, 2)
-        store_results(1, 2, PACK)
+        store_results(1)
         group(nc.vector.tensor_copy, y_grouped[1], y[1], slice(SCALAR_RESULT_COLS, QUARTER))
         group(nc.scalar.copy, y_grouped[1], y[1], slice(0, SCALAR_RESULT_COLS))
         group(nc.vector.tensor_copy, y_grouped[1], y[1], right)

@@ -24,8 +24,8 @@ QUARTER = QUERIES // 4
 LINE = 4
 MX_ALIGN = 64
 
-SCALAR_WEIGHT_COLS = (96, 64)
 SCALAR_RESULT_COLS = 64
+SCALAR_WEIGHT_COLS = 64
 
 SHELF_BYTES = 4 * TOKENS
 SHELVES = (
@@ -33,7 +33,7 @@ SHELVES = (
     "v_grouped0", "v_grouped1", "v_grouped2",
 )
 BESIDE_CODES = 1024
-V_CODES_SHELF = ("plane1", "plane2", "w_raw0", "w_raw1")
+V_CODES_SHELF = ("plane1", "plane2", "w_raw0", "plane0")
 V_GROUPED_AT = (("v_grouped0", 0), ("v_grouped1", 0), ("v_grouped2", 0), ("w_raw0", BESIDE_CODES))
 
 FLOPS = 2 * FEATURES * SLOTS * QUERIES
@@ -68,9 +68,9 @@ def tile_attend_plo_wsum_f_topk_kernel(tc, vT, wT, gn, offs, out_0, out_1, out_2
         nc.sync.dma_start(offsets[:], offs)
         for t in range(1, PACK):
             nc.sync.dma_start(out=planes[t][:], in_=v_rows[:, t, :])
-        for h in range(2):
-            nc.sync.dma_start(out=w_raw[h][:], in_=w_rows[:, :, halves[h]])
+        nc.sync.dma_start(out=w_raw[0][:], in_=w_rows[:, :, halves[0]])
         nc.sync.dma_start(out=gains[:], in_=gn[0].rearrange("(p t) o -> p (t o)", t=PACK))
+        nc.sync.dma_start(out=w_raw[1][:], in_=w_rows[:, :, halves[1]])
 
         identity = keep.tile([P, P], F32, name="identity")
         make_identity(nc, identity[:])
@@ -81,10 +81,9 @@ def tile_attend_plo_wsum_f_topk_kernel(tc, vT, wT, gn, offs, out_0, out_1, out_2
         w_codes = [keep.tile([P, HALF], U32, name=f"w_codes{h}", align_bytes=MX_ALIGN) for h in range(2)]
         w_scales = [keep.tile([P, HALF], U8, name=f"w_scales{h}", align_bytes=MX_ALIGN) for h in range(2)]
         y = [keep.tile([P, PACK, HALF], F32, name=f"y{h}") for h in range(2)]
-        y_grouped = [keep.tile([P, HALF, PACK], BF16, name=f"y_grouped{h}", align_bytes=MX_ALIGN) for h in range(2)]
         y_codes = [keep.tile([P, HALF], U32, name=f"y_codes{h}", align_bytes=MX_ALIGN) for h in range(2)]
         y_scales = keep.tile([P, QUERIES], U8, name="y_scales", align_bytes=MX_ALIGN)
-        turned, v_grouped, v_codes, w_grouped = {}, {}, {}, {}
+        turned, v_grouped, v_codes, w_grouped, y_grouped = {}, {}, {}, {}, {}
 
         def group(copy, grouped, rows, cols):
             copy(
@@ -92,16 +91,11 @@ def tile_attend_plo_wsum_f_topk_kernel(tc, vT, wT, gn, offs, out_0, out_1, out_2
                 in_=rows[:, :, cols].rearrange("p j (c i) -> p c j i", i=LINE),
             )
 
-        def group_weights(h):
-            w_grouped[h] = on_shelf([P, HALF, PACK], BF16, f"w_grouped{h}", f"w_grouped{h}")
-            group(nc.scalar.copy, w_grouped[h], w_raw[h], slice(0, SCALAR_WEIGHT_COLS[h]))
-            group(nc.vector.tensor_copy, w_grouped[h], w_raw[h], slice(SCALAR_WEIGHT_COLS[h], HALF))
-
-        def quantize_weights(h):
+        def quantize_weights(h, cols):
             nc.vector.quantize_mx(
-                out=w_codes[h][:].bitcast(FP8X4),
-                scales=w_scales[h][:],
-                in_=w_grouped[h][:].rearrange("s q j -> s (q j)"),
+                out=w_codes[h][:, cols].bitcast(FP8X4),
+                scales=w_scales[h][:, cols],
+                in_=w_grouped[h][:, cols, :].rearrange("s q j -> s (q j)"),
             )
 
         def gather_and_turn(t):
@@ -164,28 +158,41 @@ def tile_attend_plo_wsum_f_topk_kernel(tc, vT, wT, gn, offs, out_0, out_1, out_2
         quantize_values(1)
         gather_and_turn(LAST)
 
-        group_weights(0)
+        w_grouped[0] = on_shelf([P, HALF, PACK], BF16, "w_grouped0", "w_grouped0")
+        group(nc.scalar.copy, w_grouped[0], w_raw[0], slice(0, SCALAR_WEIGHT_COLS))
+        group(nc.vector.tensor_copy, w_grouped[0], w_raw[0], slice(SCALAR_WEIGHT_COLS, QUARTER))
+        group(nc.vector.tensor_copy, w_grouped[0], w_raw[0], right)
         group_values(LAST)
+        quantize_weights(0, left)
+        quantize_weights(0, right)
         quantize_values(2)
-        quantize_weights(0)
-        group_weights(1)
         quantize_values(LAST)
-        quantize_weights(1)
+        w_grouped[1] = on_shelf([P, HALF, PACK], BF16, "w_grouped1", "w_grouped0")
+        for cols in (left, right):
+            group(nc.vector.tensor_copy, w_grouped[1], w_raw[1], cols)
+        for cols in (left, right):
+            quantize_weights(1, cols)
 
         multiply(0, 0, left)
         multiply(0, 0, right)
         for t in range(1, PACK):
             multiply(t, 0, whole)
         store_results(0)
-        group(nc.vector.tensor_copy, y_grouped[0], y[0], whole)
-        quantize_results(0, whole)
+        y_grouped[0] = on_shelf([P, HALF, PACK], BF16, "y_grouped0", "w_grouped0")
+        for cols in (left, right):
+            group(nc.vector.tensor_copy, y_grouped[0], y[0], cols)
+        for cols in (left, right):
+            quantize_results(0, cols)
         store_codes(0)
 
-        for t in range(LAST):
+        multiply(0, 1, left)
+        multiply(0, 1, right)
+        for t in range(1, LAST):
             multiply(t, 1, whole)
         multiply(LAST, 1, left)
         multiply(LAST, 1, right)
         store_results(1)
+        y_grouped[1] = on_shelf([P, HALF, PACK], BF16, "y_grouped1", "w_grouped1")
         group(nc.vector.tensor_copy, y_grouped[1], y[1], slice(SCALAR_RESULT_COLS, QUARTER))
         group(nc.scalar.copy, y_grouped[1], y[1], slice(0, SCALAR_RESULT_COLS))
         group(nc.vector.tensor_copy, y_grouped[1], y[1], right)

@@ -21,6 +21,7 @@ FEATURES = 512
 QUERIES = 512
 HALF = QUERIES // 2
 QUARTER = QUERIES // 4
+AHEAD = 32
 LINE = 4
 MX_ALIGN = 64
 
@@ -61,16 +62,17 @@ def tile_attend_plo_wsum_f_topk_kernel(tc, vT, wT, gn, offs, out_0, out_1, out_2
 
         offsets = keep.tile([P, SLOTS // 16], U16, name="offsets")
         gains = keep.tile([P, PACK], F32, name="gains")
-        w_raw = [on_shelf([P, PACK, HALF], F32, f"w_raw{h}", f"w_raw{h}") for h in range(2)]
+        loads = (slice(0, HALF + AHEAD), slice(HALF + AHEAD, QUERIES))
+        w_raw = [on_shelf([P, PACK, loads[h].stop - loads[h].start], F32, f"w_raw{h}", f"w_raw{h}") for h in range(2)]
         planes = [on_shelf([P, TOKENS], F32, f"plane{t}", f"plane{t}") for t in range(PACK)]
 
         nc.sync.dma_start(out=planes[0][:], in_=v_rows[:, 0, :])
         nc.sync.dma_start(offsets[:], offs)
         for t in range(1, PACK):
             nc.sync.dma_start(out=planes[t][:], in_=v_rows[:, t, :])
-        nc.sync.dma_start(out=w_raw[0][:], in_=w_rows[:, :, halves[0]])
+        nc.sync.dma_start(out=w_raw[0][:], in_=w_rows[:, :, loads[0]])
         nc.sync.dma_start(out=gains[:], in_=gn[0].rearrange("(p t) o -> p (t o)", t=PACK))
-        nc.sync.dma_start(out=w_raw[1][:], in_=w_rows[:, :, halves[1]])
+        nc.sync.dma_start(out=w_raw[1][:], in_=w_rows[:, :, loads[1]])
 
         identity = keep.tile([P, P], F32, name="identity")
         make_identity(nc, identity[:])
@@ -85,10 +87,10 @@ def tile_attend_plo_wsum_f_topk_kernel(tc, vT, wT, gn, offs, out_0, out_1, out_2
         y_scales = keep.tile([P, QUERIES], U8, name="y_scales", align_bytes=MX_ALIGN)
         turned, v_grouped, v_codes, w_grouped, y_grouped = {}, {}, {}, {}, {}
 
-        def group(copy, grouped, rows, cols):
+        def group(copy, grouped, rows, cols, shift=0):
             copy(
                 out=grouped[:, cols, :].rearrange("p (c i) j -> p c j i", i=LINE),
-                in_=rows[:, :, cols].rearrange("p j (c i) -> p c j i", i=LINE),
+                in_=rows[:, :, cols.start + shift : cols.stop + shift].rearrange("p j (c i) -> p c j i", i=LINE),
             )
 
         def quantize_weights(h, cols):
@@ -162,14 +164,15 @@ def tile_attend_plo_wsum_f_topk_kernel(tc, vT, wT, gn, offs, out_0, out_1, out_2
         group(nc.scalar.copy, w_grouped[0], w_raw[0], slice(0, SCALAR_WEIGHT_COLS))
         group(nc.vector.tensor_copy, w_grouped[0], w_raw[0], slice(SCALAR_WEIGHT_COLS, QUARTER))
         group(nc.vector.tensor_copy, w_grouped[0], w_raw[0], right)
+        w_grouped[1] = on_shelf([P, HALF, PACK], BF16, "w_grouped1", "w_grouped1")
+        group(nc.scalar.copy, w_grouped[1], w_raw[0], slice(0, AHEAD), HALF)
         group_values(LAST)
         quantize_weights(0, left)
         quantize_weights(0, right)
         quantize_values(2)
         quantize_values(LAST)
-        w_grouped[1] = on_shelf([P, HALF, PACK], BF16, "w_grouped1", "w_grouped0")
-        for cols in (left, right):
-            group(nc.vector.tensor_copy, w_grouped[1], w_raw[1], cols)
+        for cols in (slice(AHEAD, QUARTER), right):
+            group(nc.vector.tensor_copy, w_grouped[1], w_raw[1], cols, -AHEAD)
         for cols in (left, right):
             quantize_weights(1, cols)
 
@@ -178,7 +181,7 @@ def tile_attend_plo_wsum_f_topk_kernel(tc, vT, wT, gn, offs, out_0, out_1, out_2
         for t in range(1, PACK):
             multiply(t, 0, whole)
         store_results(0)
-        y_grouped[0] = on_shelf([P, HALF, PACK], BF16, "y_grouped0", "w_grouped0")
+        y_grouped[0] = on_shelf([P, HALF, PACK], BF16, "y_grouped0", "w_grouped1")
         for cols in (left, right):
             group(nc.vector.tensor_copy, y_grouped[0], y[0], cols)
         for cols in (left, right):
@@ -192,7 +195,7 @@ def tile_attend_plo_wsum_f_topk_kernel(tc, vT, wT, gn, offs, out_0, out_1, out_2
         multiply(LAST, 1, left)
         multiply(LAST, 1, right)
         store_results(1)
-        y_grouped[1] = on_shelf([P, HALF, PACK], BF16, "y_grouped1", "w_grouped1")
+        y_grouped[1] = on_shelf([P, HALF, PACK], BF16, "y_grouped1", "w_grouped0")
         group(nc.vector.tensor_copy, y_grouped[1], y[1], slice(SCALAR_RESULT_COLS, QUARTER))
         group(nc.scalar.copy, y_grouped[1], y[1], slice(0, SCALAR_RESULT_COLS))
         group(nc.vector.tensor_copy, y_grouped[1], y[1], right)

@@ -22,7 +22,7 @@ QUERIES = 512
 HALF = QUERIES // 2
 QUARTER = QUERIES // 4
 AHEAD = 32
-LINE = 4
+LINE = 2
 MX_ALIGN = 64
 
 SCALAR_RESULT_COLS = 64

@@ -11,6 +11,7 @@ U16 = mybir.dt.uint16
 U8 = mybir.dt.uint8
 FP8X4 = mybir.dt.float8_e4m3fn_x4
 SILU = mybir.ActivationFunctionType.Silu
+COPY = mybir.ActivationFunctionType.Copy
 
 P = 128
 PACK = 4
@@ -21,20 +22,20 @@ FEATURES = 512
 QUERIES = 512
 HALF = QUERIES // 2
 QUARTER = QUERIES // 4
-AHEAD = 32
 LINE = 2
 MX_ALIGN = 64
 
-SCALAR_RESULT_COLS = 64
+SCALAR_RESULT_COLS = 48
 SCALAR_WEIGHT_COLS = 64
+VECTOR_SLOTS = 320
 
 SHELF_BYTES = 4 * TOKENS
 SHELVES = (
-    "plane0", "plane1", "plane2", "plane3", "w_raw0", "w_raw1", "w_grouped0", "w_grouped1",
-    "v_grouped0", "v_grouped1", "v_grouped2",
+    "plane0", "plane1", "plane2", "plane3", "w_raw0", "w_raw1", "w_raw2", "w_raw3",
+    "w_grouped0", "w_grouped1", "w_grouped2", "w_grouped3", "v_grouped0", "v_grouped1", "v_grouped2", "spare",
 )
 BESIDE_CODES = 1024
-V_CODES_SHELF = ("plane1", "plane2", "w_raw0", "plane0")
+V_CODES_SHELF = (("plane1", 0), ("plane2", 0), ("w_raw1", 0), ("w_raw1", BESIDE_CODES))
 V_GROUPED_AT = (("v_grouped0", 0), ("v_grouped1", 0), ("v_grouped2", 0), ("w_raw0", BESIDE_CODES))
 
 FLOPS = 2 * FEATURES * SLOTS * QUERIES
@@ -62,17 +63,18 @@ def tile_attend_plo_wsum_f_topk_kernel(tc, vT, wT, gn, offs, out_0, out_1, out_2
 
         offsets = keep.tile([P, SLOTS // 16], U16, name="offsets")
         gains = keep.tile([P, PACK], F32, name="gains")
-        loads = (slice(0, HALF + AHEAD), slice(HALF + AHEAD, QUERIES))
-        w_raw = [on_shelf([P, PACK, loads[h].stop - loads[h].start], F32, f"w_raw{h}", f"w_raw{h}") for h in range(2)]
+        quarters = [slice(k * QUARTER, (k + 1) * QUARTER) for k in range(4)]
+        w_raw = [on_shelf([P, PACK, QUARTER], F32, f"w_raw{k}", f"w_raw{k}") for k in range(4)]
         planes = [on_shelf([P, TOKENS], F32, f"plane{t}", f"plane{t}") for t in range(PACK)]
 
         nc.sync.dma_start(out=planes[0][:], in_=v_rows[:, 0, :])
         nc.sync.dma_start(offsets[:], offs)
         for t in range(1, PACK):
             nc.sync.dma_start(out=planes[t][:], in_=v_rows[:, t, :])
-        nc.sync.dma_start(out=w_raw[0][:], in_=w_rows[:, :, loads[0]])
+        nc.sync.dma_start(out=w_raw[0][:], in_=w_rows[:, :, quarters[0]])
         nc.sync.dma_start(out=gains[:], in_=gn[0].rearrange("(p t) o -> p (t o)", t=PACK))
-        nc.sync.dma_start(out=w_raw[1][:], in_=w_rows[:, :, loads[1]])
+        for k in range(1, 4):
+            nc.sync.dma_start(out=w_raw[k][:], in_=w_rows[:, :, quarters[k]])
 
         identity = keep.tile([P, P], F32, name="identity")
         make_identity(nc, identity[:])
@@ -93,16 +95,26 @@ def tile_attend_plo_wsum_f_topk_kernel(tc, vT, wT, gn, offs, out_0, out_1, out_2
                 in_=rows[:, :, cols.start + shift : cols.stop + shift].rearrange("p j (c i) -> p c j i", i=LINE),
             )
 
-        def quantize_weights(h, cols):
+        def round_weights(k, scalar_cols):
+            w_grouped[k] = on_shelf([P, QUARTER, PACK], BF16, f"w_grouped{k}", f"w_grouped{k}")
+            if scalar_cols:
+                group(nc.scalar.copy, w_grouped[k], w_raw[k], slice(0, scalar_cols))
+            group(nc.vector.tensor_copy, w_grouped[k], w_raw[k], slice(scalar_cols, QUARTER))
+
+        def quantize_weights(k):
+            h, cols = k // 2, (left, right)[k % 2]
             nc.vector.quantize_mx(
                 out=w_codes[h][:, cols].bitcast(FP8X4),
                 scales=w_scales[h][:, cols],
-                in_=w_grouped[h][:, cols, :].rearrange("s q j -> s (q j)"),
+                in_=w_grouped[k][:].rearrange("s q j -> s (q j)"),
             )
 
         def gather_and_turn(t):
             picked = keep.tile([P, SLOTS], BF16, name=f"picked{t}", align_bytes=MX_ALIGN)
-            nc.vector.tensor_copy(picked[:], planes[t][:].indirect(offsets[:]))
+            cut = VECTOR_SLOTS if t >= 2 else SLOTS
+            nc.vector.tensor_copy(picked[:, :cut], planes[t][:].indirect(offsets[:, : cut // 16]))
+            if cut < SLOTS:
+                nc.scalar.activation(out=picked[:, cut:], in_=planes[t][:].indirect(offsets[:, cut // 16 :]), func=COPY)
             slot_pairs = picked[:].bitcast(F32)
             turned[t] = turn.tile([P, 2, P], F32, name="turned")
             for u in range(2):
@@ -116,7 +128,7 @@ def tile_attend_plo_wsum_f_topk_kernel(tc, vT, wT, gn, offs, out_0, out_1, out_2
             )
 
         def quantize_values(t):
-            v_codes[t] = on_shelf([P, P], U32, f"v_codes{t}", V_CODES_SHELF[t])
+            v_codes[t] = on_shelf([P, P], U32, f"v_codes{t}", *V_CODES_SHELF[t])
             nc.vector.quantize_mx(
                 out=v_codes[t][:].bitcast(FP8X4),
                 scales=v_scales[t][:],
@@ -151,55 +163,46 @@ def tile_attend_plo_wsum_f_topk_kernel(tc, vT, wT, gn, offs, out_0, out_1, out_2
         def store_codes(h):
             nc.sync.dma_start(out=y_words[:, halves[h]], in_=y_codes[h][:].bitcast(I32))
 
-        for t in range(2):
+        for t in range(LAST):
             gather_and_turn(t)
             group_values(t)
-        quantize_values(0)
-        gather_and_turn(2)
-        group_values(2)
-        quantize_values(1)
+            if t:
+                quantize_values(t - 1)
         gather_and_turn(LAST)
 
-        w_grouped[0] = on_shelf([P, HALF, PACK], BF16, "w_grouped0", "w_grouped0")
-        group(nc.scalar.copy, w_grouped[0], w_raw[0], slice(0, SCALAR_WEIGHT_COLS))
-        group(nc.vector.tensor_copy, w_grouped[0], w_raw[0], slice(SCALAR_WEIGHT_COLS, QUARTER))
-        group(nc.vector.tensor_copy, w_grouped[0], w_raw[0], right)
-        w_grouped[1] = on_shelf([P, HALF, PACK], BF16, "w_grouped1", "w_grouped1")
-        group(nc.scalar.copy, w_grouped[1], w_raw[0], slice(0, AHEAD), HALF)
+        round_weights(0, SCALAR_WEIGHT_COLS)
         group_values(LAST)
-        quantize_weights(0, left)
-        quantize_weights(0, right)
+        quantize_weights(0)
+        round_weights(1, 0)
         quantize_values(2)
+        quantize_weights(1)
+        round_weights(2, 0)
         quantize_values(LAST)
-        for cols in (slice(AHEAD, QUARTER), right):
-            group(nc.vector.tensor_copy, w_grouped[1], w_raw[1], cols, -AHEAD)
-        for cols in (left, right):
-            quantize_weights(1, cols)
+        quantize_weights(2)
+        round_weights(3, 0)
+        quantize_weights(3)
 
-        multiply(0, 0, left)
-        multiply(0, 0, right)
-        for t in range(1, PACK):
-            multiply(t, 0, whole)
+        for cols in (left, right):
+            for t in range(LAST):
+                multiply(t, 0, cols)
+        multiply(LAST, 0, whole)
         store_results(0)
-        y_grouped[0] = on_shelf([P, HALF, PACK], BF16, "y_grouped0", "w_grouped1")
+        y_grouped[0] = on_shelf([P, HALF, PACK], BF16, "y_grouped0", "w_grouped3")
         for cols in (left, right):
             group(nc.vector.tensor_copy, y_grouped[0], y[0], cols)
         for cols in (left, right):
             quantize_results(0, cols)
         store_codes(0)
 
-        multiply(0, 1, left)
-        multiply(0, 1, right)
-        for t in range(1, LAST):
-            multiply(t, 1, whole)
-        multiply(LAST, 1, left)
-        multiply(LAST, 1, right)
+        for cols in (left, right):
+            for t in range(PACK):
+                multiply(t, 1, cols)
         store_results(1)
-        y_grouped[1] = on_shelf([P, HALF, PACK], BF16, "y_grouped1", "w_grouped0")
-        group(nc.vector.tensor_copy, y_grouped[1], y[1], slice(SCALAR_RESULT_COLS, QUARTER))
-        group(nc.scalar.copy, y_grouped[1], y[1], slice(0, SCALAR_RESULT_COLS))
-        group(nc.vector.tensor_copy, y_grouped[1], y[1], right)
+        y_grouped[1] = on_shelf([P, HALF, PACK], BF16, "y_grouped1", "spare")
+        group(nc.vector.tensor_copy, y_grouped[1], y[1], left)
         quantize_results(1, left)
+        group(nc.vector.tensor_copy, y_grouped[1], y[1], slice(QUARTER, HALF - SCALAR_RESULT_COLS))
+        group(nc.scalar.copy, y_grouped[1], y[1], slice(HALF - SCALAR_RESULT_COLS, HALF))
         quantize_results(1, right)
         store_codes(1)
 

@@ -35,7 +35,7 @@ SHELVES = (
     "w_grouped0", "w_grouped1", "w_grouped2", "w_grouped3", "v_grouped0", "v_grouped1", "v_grouped2", "spare",
 )
 BESIDE_CODES = 1024
-V_CODES_SHELF = (("plane1", 0), ("plane2", 0), ("w_raw1", 0), ("w_raw1", BESIDE_CODES))
+V_CODES_SHELF = (("plane1", 0), ("plane2", 0), ("w_raw0", 0), ("w_raw1", 0))
 V_GROUPED_AT = (("v_grouped0", 0), ("v_grouped1", 0), ("v_grouped2", 0), ("w_raw0", BESIDE_CODES))
 
 FLOPS = 2 * FEATURES * SLOTS * QUERIES
@@ -71,10 +71,10 @@ def tile_attend_plo_wsum_f_topk_kernel(tc, vT, wT, gn, offs, out_0, out_1, out_2
         nc.sync.dma_start(offsets[:], offs)
         for t in range(1, PACK):
             nc.sync.dma_start(out=planes[t][:], in_=v_rows[:, t, :])
-        nc.sync.dma_start(out=w_raw[0][:], in_=w_rows[:, :, quarters[0]])
-        nc.sync.dma_start(out=gains[:], in_=gn[0].rearrange("(p t) o -> p (t o)", t=PACK))
-        for k in range(1, 4):
+        for k in range(4):
             nc.sync.dma_start(out=w_raw[k][:], in_=w_rows[:, :, quarters[k]])
+            if k == 0:
+                nc.sync.dma_start(out=gains[:], in_=gn[0].rearrange("(p t) o -> p (t o)", t=PACK))
 
         identity = keep.tile([P, P], F32, name="identity")
         make_identity(nc, identity[:])
@@ -194,9 +194,10 @@ def tile_attend_plo_wsum_f_topk_kernel(tc, vT, wT, gn, offs, out_0, out_1, out_2
             quantize_results(0, cols)
         store_codes(0)
 
-        for cols in (left, right):
-            for t in range(PACK):
-                multiply(t, 1, cols)
+        for pair in ((0, 1), (2, 3)):
+            for cols in (left, right):
+                for t in pair:
+                    multiply(t, 1, cols)
         store_results(1)
         y_grouped[1] = on_shelf([P, HALF, PACK], BF16, "y_grouped1", "spare")
         group(nc.vector.tensor_copy, y_grouped[1], y[1], left)

@@ -26,8 +26,8 @@ LINE = 2
 MX_ALIGN = 64
 
 SCALAR_RESULT_COLS = 48
-SCALAR_WEIGHT_COLS = 64
-VECTOR_SLOTS = 320
+SCALAR_WEIGHT_COLS = 32
+VECTOR_SLOTS = 288
 
 SHELF_BYTES = 4 * TOKENS
 SHELVES = (
@@ -35,7 +35,9 @@ SHELVES = (
     "w_grouped0", "w_grouped1", "w_grouped2", "w_grouped3", "v_grouped0", "v_grouped1", "v_grouped2", "spare",
 )
 BESIDE_CODES = 1024
-V_CODES_SHELF = (("plane1", 0), ("plane2", 0), ("w_raw0", 0), ("w_raw1", 0))
+V_CODES_SHELF = (("plane1", 0), ("plane2", 0), ("w_grouped0", 0), ("w_grouped1", 0))
+W_GROUPED_AT = (("w_grouped0", 0), ("w_grouped1", 0), ("v_grouped2", 0), ("w_raw0", BESIDE_CODES))
+Y_GROUPED_AT = (("w_raw3", 0), ("w_raw0", BESIDE_CODES), ("w_raw3", 0), ("w_raw0", BESIDE_CODES))
 V_GROUPED_AT = (("v_grouped0", 0), ("v_grouped1", 0), ("v_grouped2", 0), ("w_raw0", BESIDE_CODES))
 
 FLOPS = 2 * FEATURES * SLOTS * QUERIES
@@ -67,13 +69,15 @@ def tile_attend_plo_wsum_f_topk_kernel(tc, vT, wT, gn, offs, out_0, out_1, out_2
         w_raw = [on_shelf([P, PACK, QUARTER], F32, f"w_raw{k}", f"w_raw{k}") for k in range(4)]
         planes = [on_shelf([P, TOKENS], F32, f"plane{t}", f"plane{t}") for t in range(PACK)]
 
-        nc.sync.dma_start(out=planes[0][:], in_=v_rows[:, 0, :])
+        for first in (0, TOKENS // 2):
+            part = slice(first, first + TOKENS // 2)
+            nc.sync.dma_start(out=planes[0][:, part], in_=v_rows[:, 0, part])
         nc.sync.dma_start(offsets[:], offs)
         for t in range(1, PACK):
             nc.sync.dma_start(out=planes[t][:], in_=v_rows[:, t, :])
         for k in range(4):
             nc.sync.dma_start(out=w_raw[k][:], in_=w_rows[:, :, quarters[k]])
-            if k == 0:
+            if k == 1:
                 nc.sync.dma_start(out=gains[:], in_=gn[0].rearrange("(p t) o -> p (t o)", t=PACK))
 
         identity = keep.tile([P, P], F32, name="identity")
@@ -96,7 +100,7 @@ def tile_attend_plo_wsum_f_topk_kernel(tc, vT, wT, gn, offs, out_0, out_1, out_2
             )
 
         def round_weights(k, scalar_cols):
-            w_grouped[k] = on_shelf([P, QUARTER, PACK], BF16, f"w_grouped{k}", f"w_grouped{k}")
+            w_grouped[k] = on_shelf([P, QUARTER, PACK], BF16, f"w_grouped{k}", *W_GROUPED_AT[k])
             if scalar_cols:
                 group(nc.scalar.copy, w_grouped[k], w_raw[k], slice(0, scalar_cols))
             group(nc.vector.tensor_copy, w_grouped[k], w_raw[k], slice(scalar_cols, QUARTER))
@@ -148,17 +152,24 @@ def tile_attend_plo_wsum_f_topk_kernel(tc, vT, wT, gn, offs, out_0, out_1, out_2
             )
             nc.scalar.activation(out=y[h][:, t, cols], in_=acc[:], func=SILU, scale=gains[:, t : t + 1])
 
-        def store_results(h):
-            for first in (0, 2):
-                nc.sync.dma_start(out=y_rows[:, first : first + 2, halves[h]], in_=y[h][:, first : first + 2, :])
+        def store_results(h, ts, cols):
+            first = halves[h].start
+            nc.sync.dma_start(out=y_rows[:, ts, first + cols.start : first + cols.stop], in_=y[h][:, ts, cols])
 
         def quantize_results(h, cols):
             first = halves[h].start
             nc.vector.quantize_mx(
                 out=y_codes[h][:, cols].bitcast(FP8X4),
                 scales=y_scales[:, first + cols.start : first + cols.stop],
-                in_=y_grouped[h][:, cols, :].rearrange("p q t -> p (q t)"),
+                in_=y_grouped[2 * h + cols.start // QUARTER][:].rearrange("p q t -> p (q t)"),
             )
+
+        def round_results(h, cols, scalar_cols):
+            k = 2 * h + cols.start // QUARTER
+            y_grouped[k] = on_shelf([P, QUARTER, PACK], BF16, f"y_grouped{k}", *Y_GROUPED_AT[k])
+            group(nc.vector.tensor_copy, y_grouped[k], y[h], slice(0, QUARTER - scalar_cols), cols.start)
+            if scalar_cols:
+                group(nc.scalar.copy, y_grouped[k], y[h], slice(QUARTER - scalar_cols, QUARTER), cols.start)
 
         def store_codes(h):
             nc.sync.dma_start(out=y_words[:, halves[h]], in_=y_codes[h][:].bitcast(I32))
@@ -185,25 +196,21 @@ def tile_attend_plo_wsum_f_topk_kernel(tc, vT, wT, gn, offs, out_0, out_1, out_2
         for cols in (left, right):
             for t in range(LAST):
                 multiply(t, 0, cols)
+            store_results(0, slice(0, LAST), cols)
         multiply(LAST, 0, whole)
-        store_results(0)
-        y_grouped[0] = on_shelf([P, HALF, PACK], BF16, "y_grouped0", "w_grouped3")
+        store_results(0, slice(LAST, PACK), whole)
         for cols in (left, right):
-            group(nc.vector.tensor_copy, y_grouped[0], y[0], cols)
+            round_results(0, cols, 0)
         for cols in (left, right):
             quantize_results(0, cols)
         store_codes(0)
 
-        for pair in ((0, 1), (2, 3)):
-            for cols in (left, right):
-                for t in pair:
-                    multiply(t, 1, cols)
-        store_results(1)
-        y_grouped[1] = on_shelf([P, HALF, PACK], BF16, "y_grouped1", "spare")
-        group(nc.vector.tensor_copy, y_grouped[1], y[1], left)
+        for cols in (left, right):
+            for t in range(PACK):
+                multiply(t, 1, cols)
+            store_results(1, slice(0, PACK), cols)
+            round_results(1, cols, 0 if cols is left else SCALAR_RESULT_COLS)
         quantize_results(1, left)
-        group(nc.vector.tensor_copy, y_grouped[1], y[1], slice(QUARTER, HALF - SCALAR_RESULT_COLS))
-        group(nc.scalar.copy, y_grouped[1], y[1], slice(HALF - SCALAR_RESULT_COLS, HALF))
         quantize_results(1, right)
         store_codes(1)
 

@@ -26,7 +26,7 @@ LINE = 2
 MX_ALIGN = 64
 
 SCALAR_RESULT_COLS = 48
-SCALAR_WEIGHT_COLS = 32
+SCALAR_WEIGHT_COLS = (64, 48)
 VECTOR_SLOTS = 288
 
 SHELF_BYTES = 4 * TOKENS
@@ -35,10 +35,10 @@ SHELVES = (
     "w_grouped0", "w_grouped1", "w_grouped2", "w_grouped3", "v_grouped0", "v_grouped1", "v_grouped2", "spare",
 )
 BESIDE_CODES = 1024
-V_CODES_SHELF = (("plane1", 0), ("plane2", 0), ("w_grouped0", 0), ("w_grouped1", 0))
-W_GROUPED_AT = (("w_grouped0", 0), ("w_grouped1", 0), ("v_grouped2", 0), ("w_raw0", BESIDE_CODES))
-Y_GROUPED_AT = (("w_raw3", 0), ("w_raw0", BESIDE_CODES), ("w_raw3", 0), ("w_raw0", BESIDE_CODES))
-V_GROUPED_AT = (("v_grouped0", 0), ("v_grouped1", 0), ("v_grouped2", 0), ("w_raw0", BESIDE_CODES))
+V_CODES_SHELF = (("plane1", 0), ("plane2", 0), ("w_grouped0", 0), ("v_grouped2", 0))
+W_GROUPED_AT = (("w_grouped0", 0), ("w_grouped1", 0), ("w_grouped1", 0), ("w_raw2", 0))
+Y_GROUPED_AT = (("w_raw3", 0), ("w_raw2", 0), ("w_raw3", 0), ("w_raw2", 0))
+V_GROUPED_AT = (("v_grouped0", 0), ("v_grouped1", 0), ("v_grouped2", 0), ("w_raw1", 0))
 
 FLOPS = 2 * FEATURES * SLOTS * QUERIES
 
@@ -69,9 +69,7 @@ def tile_attend_plo_wsum_f_topk_kernel(tc, vT, wT, gn, offs, out_0, out_1, out_2
         w_raw = [on_shelf([P, PACK, QUARTER], F32, f"w_raw{k}", f"w_raw{k}") for k in range(4)]
         planes = [on_shelf([P, TOKENS], F32, f"plane{t}", f"plane{t}") for t in range(PACK)]
 
-        for first in (0, TOKENS // 2):
-            part = slice(first, first + TOKENS // 2)
-            nc.sync.dma_start(out=planes[0][:, part], in_=v_rows[:, 0, part])
+        nc.sync.dma_start(out=planes[0][:], in_=v_rows[:, 0, :])
         nc.sync.dma_start(offsets[:], offs)
         for t in range(1, PACK):
             nc.sync.dma_start(out=planes[t][:], in_=v_rows[:, t, :])
@@ -181,34 +179,38 @@ def tile_attend_plo_wsum_f_topk_kernel(tc, vT, wT, gn, offs, out_0, out_1, out_2
                 quantize_values(t - 1)
         gather_and_turn(LAST)
 
-        round_weights(0, SCALAR_WEIGHT_COLS)
-        group_values(LAST)
+        round_weights(0, SCALAR_WEIGHT_COLS[0])
         quantize_weights(0)
-        round_weights(1, 0)
+        round_weights(1, SCALAR_WEIGHT_COLS[1])
+        group_values(LAST)
         quantize_values(2)
         quantize_weights(1)
-        round_weights(2, 0)
         quantize_values(LAST)
+        round_weights(2, 0)
         quantize_weights(2)
         round_weights(3, 0)
         quantize_weights(3)
 
         for cols in (left, right):
-            for t in range(LAST):
+            multiply(0, 0, cols)
+            if cols is left:
+                store_results(0, slice(0, 1), cols)
+            for t in range(1, LAST):
                 multiply(t, 0, cols)
-            store_results(0, slice(0, LAST), cols)
+            store_results(0, slice(1 if cols is left else 0, LAST), cols)
         multiply(LAST, 0, whole)
         store_results(0, slice(LAST, PACK), whole)
         for cols in (left, right):
             round_results(0, cols, 0)
         for cols in (left, right):
             quantize_results(0, cols)
-        store_codes(0)
 
         for cols in (left, right):
             for t in range(PACK):
                 multiply(t, 1, cols)
             store_results(1, slice(0, PACK), cols)
+            if cols is left:
+                store_codes(0)
             round_results(1, cols, 0 if cols is left else SCALAR_RESULT_COLS)
         quantize_results(1, left)
         quantize_results(1, right)

@@ -25,20 +25,21 @@ QUARTER = QUERIES // 4
 LINE = 2
 MX_ALIGN = 64
 
-SCALAR_RESULT_COLS = 48
-SCALAR_WEIGHT_COLS = (64, 48)
+FIRST_SHARED_PLANE = 2
 VECTOR_SLOTS = 288
+SCALAR_WEIGHT_COLS = (64, 48, 0, 0)
+SCALAR_RESULT_COLS = 48
 
 SHELF_BYTES = 4 * TOKENS
 SHELVES = (
     "plane0", "plane1", "plane2", "plane3", "w_raw0", "w_raw1", "w_raw2", "w_raw3",
-    "w_grouped0", "w_grouped1", "w_grouped2", "w_grouped3", "v_grouped0", "v_grouped1", "v_grouped2", "spare",
+    "w_grouped0", "w_grouped1", "v_grouped0", "v_grouped1", "v_grouped2",
 )
-BESIDE_CODES = 1024
-V_CODES_SHELF = (("plane1", 0), ("plane2", 0), ("w_grouped0", 0), ("v_grouped2", 0))
-W_GROUPED_AT = (("w_grouped0", 0), ("w_grouped1", 0), ("w_grouped1", 0), ("w_raw2", 0))
-Y_GROUPED_AT = (("w_raw3", 0), ("w_raw2", 0), ("w_raw3", 0), ("w_raw2", 0))
-V_GROUPED_AT = (("v_grouped0", 0), ("v_grouped1", 0), ("v_grouped2", 0), ("w_raw1", 0))
+BESIDE_CODES = 4 * P
+V_GROUPED_AT = (("v_grouped0", 0), ("v_grouped1", 0), ("v_grouped2", 0), ("w_grouped0", BESIDE_CODES))
+V_CODES_ON = ("plane1", "plane2", "w_grouped0", "v_grouped2")
+W_GROUPED_ON = ("w_grouped0", "w_grouped1", "w_grouped1", "w_raw2")
+Y_GROUPED_ON = ("w_raw3", "w_raw2", "w_raw3", "w_raw2")
 
 FLOPS = 2 * FEATURES * SLOTS * QUERIES
 
@@ -97,8 +98,9 @@ def tile_attend_plo_wsum_f_topk_kernel(tc, vT, wT, gn, offs, out_0, out_1, out_2
                 in_=rows[:, :, cols.start + shift : cols.stop + shift].rearrange("p j (c i) -> p c j i", i=LINE),
             )
 
-        def round_weights(k, scalar_cols):
-            w_grouped[k] = on_shelf([P, QUARTER, PACK], BF16, f"w_grouped{k}", *W_GROUPED_AT[k])
+        def round_weights(k):
+            scalar_cols = SCALAR_WEIGHT_COLS[k]
+            w_grouped[k] = on_shelf([P, QUARTER, PACK], BF16, f"w_grouped{k}", W_GROUPED_ON[k])
             if scalar_cols:
                 group(nc.scalar.copy, w_grouped[k], w_raw[k], slice(0, scalar_cols))
             group(nc.vector.tensor_copy, w_grouped[k], w_raw[k], slice(scalar_cols, QUARTER))
@@ -113,7 +115,7 @@ def tile_attend_plo_wsum_f_topk_kernel(tc, vT, wT, gn, offs, out_0, out_1, out_2
 
         def gather_and_turn(t):
             picked = keep.tile([P, SLOTS], BF16, name=f"picked{t}", align_bytes=MX_ALIGN)
-            cut = VECTOR_SLOTS if t >= 2 else SLOTS
+            cut = VECTOR_SLOTS if t >= FIRST_SHARED_PLANE else SLOTS
             nc.vector.tensor_copy(picked[:, :cut], planes[t][:].indirect(offsets[:, : cut // 16]))
             if cut < SLOTS:
                 nc.scalar.activation(out=picked[:, cut:], in_=planes[t][:].indirect(offsets[:, cut // 16 :]), func=COPY)
@@ -130,7 +132,7 @@ def tile_attend_plo_wsum_f_topk_kernel(tc, vT, wT, gn, offs, out_0, out_1, out_2
             )
 
         def quantize_values(t):
-            v_codes[t] = on_shelf([P, P], U32, f"v_codes{t}", *V_CODES_SHELF[t])
+            v_codes[t] = on_shelf([P, P], U32, f"v_codes{t}", V_CODES_ON[t])
             nc.vector.quantize_mx(
                 out=v_codes[t][:].bitcast(FP8X4),
                 scales=v_scales[t][:],
@@ -162,9 +164,9 @@ def tile_attend_plo_wsum_f_topk_kernel(tc, vT, wT, gn, offs, out_0, out_1, out_2
                 in_=y_grouped[2 * h + cols.start // QUARTER][:].rearrange("p q t -> p (q t)"),
             )
 
-        def round_results(h, cols, scalar_cols):
+        def round_results(h, cols, scalar_cols=0):
             k = 2 * h + cols.start // QUARTER
-            y_grouped[k] = on_shelf([P, QUARTER, PACK], BF16, f"y_grouped{k}", *Y_GROUPED_AT[k])
+            y_grouped[k] = on_shelf([P, QUARTER, PACK], BF16, f"y_grouped{k}", Y_GROUPED_ON[k])
             group(nc.vector.tensor_copy, y_grouped[k], y[h], slice(0, QUARTER - scalar_cols), cols.start)
             if scalar_cols:
                 group(nc.scalar.copy, y_grouped[k], y[h], slice(QUARTER - scalar_cols, QUARTER), cols.start)
@@ -179,41 +181,44 @@ def tile_attend_plo_wsum_f_topk_kernel(tc, vT, wT, gn, offs, out_0, out_1, out_2
                 quantize_values(t - 1)
         gather_and_turn(LAST)
 
-        round_weights(0, SCALAR_WEIGHT_COLS[0])
+        round_weights(0)
         quantize_weights(0)
-        round_weights(1, SCALAR_WEIGHT_COLS[1])
+        round_weights(1)
         group_values(LAST)
         quantize_values(2)
         quantize_weights(1)
         quantize_values(LAST)
-        round_weights(2, 0)
-        quantize_weights(2)
-        round_weights(3, 0)
-        quantize_weights(3)
+        for k in (2, 3):
+            round_weights(k)
+            quantize_weights(k)
 
-        for cols in (left, right):
-            multiply(0, 0, cols)
-            if cols is left:
-                store_results(0, slice(0, 1), cols)
-            for t in range(1, LAST):
-                multiply(t, 0, cols)
-            store_results(0, slice(1 if cols is left else 0, LAST), cols)
+        multiply(0, 0, left)
+        store_results(0, slice(0, 1), left)
+        for t in range(1, LAST):
+            multiply(t, 0, left)
+        store_results(0, slice(1, LAST), left)
+        for t in range(LAST):
+            multiply(t, 0, right)
+        store_results(0, slice(0, LAST), right)
         multiply(LAST, 0, whole)
         store_results(0, slice(LAST, PACK), whole)
         for cols in (left, right):
-            round_results(0, cols, 0)
+            round_results(0, cols)
         for cols in (left, right):
             quantize_results(0, cols)
 
+        for t in range(PACK):
+            multiply(t, 1, left)
+        store_results(1, slice(0, PACK), left)
+        store_codes(0)
+        round_results(1, left)
+
+        for t in range(PACK):
+            multiply(t, 1, right)
+        store_results(1, slice(0, PACK), right)
+        round_results(1, right, SCALAR_RESULT_COLS)
         for cols in (left, right):
-            for t in range(PACK):
-                multiply(t, 1, cols)
-            store_results(1, slice(0, PACK), cols)
-            if cols is left:
-                store_codes(0)
-            round_results(1, cols, 0 if cols is left else SCALAR_RESULT_COLS)
-        quantize_results(1, left)
-        quantize_results(1, right)
+            quantize_results(1, cols)
         store_codes(1)
 
         for quad in range(P // 32):

from contextlib import ExitStack

import concourse.mybir as mybir
from concourse.masks import make_identity

F32 = mybir.dt.float32
BF16 = mybir.dt.bfloat16
I32 = mybir.dt.int32
U32 = mybir.dt.uint32
U16 = mybir.dt.uint16
U8 = mybir.dt.uint8
FP8X4 = mybir.dt.float8_e4m3fn_x4
SILU = mybir.ActivationFunctionType.Silu
COPY = mybir.ActivationFunctionType.Copy

P = 128
PACK = 4
LAST = PACK - 1
SLOTS = 512
TOKENS = 2048
FEATURES = 512
QUERIES = 512
HALF = QUERIES // 2
QUARTER = QUERIES // 4
LINE = 2
MX_ALIGN = 64

FIRST_SHARED_PLANE = 2
VECTOR_SLOTS = 288
SCALAR_WEIGHT_COLS = (64, 48, 0, 0)
SCALAR_RESULT_COLS = 48

SHELF_BYTES = 4 * TOKENS
SHELVES = (
    "plane0", "plane1", "plane2", "plane3", "w_raw0", "w_raw1", "w_raw2", "w_raw3",
    "w_grouped0", "w_grouped1", "v_grouped0", "v_grouped1", "v_grouped2",
)
BESIDE_CODES = 4 * P
V_GROUPED_AT = (("v_grouped0", 0), ("v_grouped1", 0), ("v_grouped2", 0), ("w_grouped0", BESIDE_CODES))
V_CODES_ON = ("plane1", "plane2", "w_grouped0", "v_grouped2")
W_GROUPED_ON = ("w_grouped0", "w_grouped1", "w_grouped1", "w_raw2")
Y_GROUPED_ON = ("w_raw3", "w_raw2", "w_raw3", "w_raw2")

FLOPS = 2 * FEATURES * SLOTS * QUERIES


def tile_attend_plo_wsum_f_topk_kernel(tc, vT, wT, gn, offs, out_0, out_1, out_2):
    nc = tc.nc
    v_rows = vT.rearrange("(p t) n -> p t n", t=PACK)
    w_rows = wT[0].rearrange("(p j) q -> p j q", j=PACK)
    y_rows = out_0.rearrange("(p t) q -> p t q", t=PACK)
    y_words = out_1[0].rearrange("p q t -> p (q t)").bitcast(I32)
    y_scale_rows = out_2[0].bitcast(I32)
    halves = (slice(0, HALF), slice(HALF, QUERIES))
    whole, left, right = slice(0, HALF), slice(0, QUARTER), slice(QUARTER, HALF)

    with ExitStack() as ctx:
        keep = ctx.enter_context(tc.tile_pool(name="keep", bufs=1))
        shelved = ctx.enter_context(tc.tile_pool(name="shelved", bufs=1))
        turn = ctx.enter_context(tc.psum_pool(name="turn", bufs=2))
        sums = ctx.enter_context(tc.psum_pool(name="sums", bufs=6))

        def on_shelf(shape, dtype, name, shelf, skip=0):
            offset = SHELVES.index(shelf) * SHELF_BYTES + skip
            return shelved.tile(shape, dtype, name=name, align_bytes=MX_ALIGN, offset=offset)

        offsets = keep.tile([P, SLOTS // 16], U16, name="offsets")
        gains = keep.tile([P, PACK], F32, name="gains")
        quarters = [slice(k * QUARTER, (k + 1) * QUARTER) for k in range(4)]
        w_raw = [on_shelf([P, PACK, QUARTER], F32, f"w_raw{k}", f"w_raw{k}") for k in range(4)]
        planes = [on_shelf([P, TOKENS], F32, f"plane{t}", f"plane{t}") for t in range(PACK)]

        nc.sync.dma_start(out=planes[0][:], in_=v_rows[:, 0, :])
        nc.sync.dma_start(offsets[:], offs)
        for t in range(1, PACK):
            nc.sync.dma_start(out=planes[t][:], in_=v_rows[:, t, :])
        for k in range(4):
            nc.sync.dma_start(out=w_raw[k][:], in_=w_rows[:, :, quarters[k]])
            if k == 1:
                nc.sync.dma_start(out=gains[:], in_=gn[0].rearrange("(p t) o -> p (t o)", t=PACK))

        identity = keep.tile([P, P], F32, name="identity")
        make_identity(nc, identity[:])
        table_warm_up = keep.tile([P, 1], F32, name="table_warm_up")
        nc.scalar.activation(out=table_warm_up[:], in_=identity[:, 0:1], func=SILU)

        v_scales = [keep.tile([P, P], U8, name=f"v_scales{t}", align_bytes=MX_ALIGN) for t in range(PACK)]
        w_codes = [keep.tile([P, HALF], U32, name=f"w_codes{h}", align_bytes=MX_ALIGN) for h in range(2)]
        w_scales = [keep.tile([P, HALF], U8, name=f"w_scales{h}", align_bytes=MX_ALIGN) for h in range(2)]
        y = [keep.tile([P, PACK, HALF], F32, name=f"y{h}") for h in range(2)]
        y_codes = [keep.tile([P, HALF], U32, name=f"y_codes{h}", align_bytes=MX_ALIGN) for h in range(2)]
        y_scales = keep.tile([P, QUERIES], U8, name="y_scales", align_bytes=MX_ALIGN)
        turned, v_grouped, v_codes, w_grouped, y_grouped = {}, {}, {}, {}, {}

        def group(copy, grouped, rows, cols, shift=0):
            copy(
                out=grouped[:, cols, :].rearrange("p (c i) j -> p c j i", i=LINE),
                in_=rows[:, :, cols.start + shift : cols.stop + shift].rearrange("p j (c i) -> p c j i", i=LINE),
            )

        def round_weights(k):
            scalar_cols = SCALAR_WEIGHT_COLS[k]
            w_grouped[k] = on_shelf([P, QUARTER, PACK], BF16, f"w_grouped{k}", W_GROUPED_ON[k])
            if scalar_cols:
                group(nc.scalar.copy, w_grouped[k], w_raw[k], slice(0, scalar_cols))
            group(nc.vector.tensor_copy, w_grouped[k], w_raw[k], slice(scalar_cols, QUARTER))

        def quantize_weights(k):
            h, cols = k // 2, (left, right)[k % 2]
            nc.vector.quantize_mx(
                out=w_codes[h][:, cols].bitcast(FP8X4),
                scales=w_scales[h][:, cols],
                in_=w_grouped[k][:].rearrange("s q j -> s (q j)"),
            )

        def gather_and_turn(t):
            picked = keep.tile([P, SLOTS], BF16, name=f"picked{t}", align_bytes=MX_ALIGN)
            cut = VECTOR_SLOTS if t >= FIRST_SHARED_PLANE else SLOTS
            nc.vector.tensor_copy(picked[:, :cut], planes[t][:].indirect(offsets[:, : cut // 16]))
            if cut < SLOTS:
                nc.scalar.activation(out=picked[:, cut:], in_=planes[t][:].indirect(offsets[:, cut // 16 :]), func=COPY)
            slot_pairs = picked[:].bitcast(F32)
            turned[t] = turn.tile([P, 2, P], F32, name="turned")
            for u in range(2):
                nc.tensor.transpose(turned[t][:, u, :], slot_pairs[:, u : SLOTS // 2 : 2], identity[:])

        def group_values(t):
            v_grouped[t] = on_shelf([P, P, PACK], BF16, f"v_grouped{t}", *V_GROUPED_AT[t])
            nc.scalar.copy(
                out=v_grouped[t][:].rearrange("s p j -> s (p j)").bitcast(F32).rearrange("s (p u) -> s p u", u=2),
                in_=turned[t][:].rearrange("s u p -> s p u"),
            )

        def quantize_values(t):
            v_codes[t] = on_shelf([P, P], U32, f"v_codes{t}", V_CODES_ON[t])
            nc.vector.quantize_mx(
                out=v_codes[t][:].bitcast(FP8X4),
                scales=v_scales[t][:],
                in_=v_grouped[t][:].rearrange("s p j -> s (p j)"),
            )

        def multiply(t, h, cols):
            acc = sums.tile([P, cols.stop - cols.start], F32, name="acc")
            nc.tensor.matmul_mx(
                out=acc[:],
                lhsT=v_codes[t][:].bitcast(FP8X4),
                lhsT_scale=v_scales[t][:],
                rhs=w_codes[h][:, cols].bitcast(FP8X4),
                rhs_scale=w_scales[h][:, cols],
                start=True,
                stop=True,
            )
            nc.scalar.activation(out=y[h][:, t, cols], in_=acc[:], func=SILU, scale=gains[:, t : t + 1])

        def store_results(h, ts, cols):
            first = halves[h].start
            nc.sync.dma_start(out=y_rows[:, ts, first + cols.start : first + cols.stop], in_=y[h][:, ts, cols])

        def quantize_results(h, cols):
            first = halves[h].start
            nc.vector.quantize_mx(
                out=y_codes[h][:, cols].bitcast(FP8X4),
                scales=y_scales[:, first + cols.start : first + cols.stop],
                in_=y_grouped[2 * h + cols.start // QUARTER][:].rearrange("p q t -> p (q t)"),
            )

        def round_results(h, cols, scalar_cols=0):
            k = 2 * h + cols.start // QUARTER
            y_grouped[k] = on_shelf([P, QUARTER, PACK], BF16, f"y_grouped{k}", Y_GROUPED_ON[k])
            group(nc.vector.tensor_copy, y_grouped[k], y[h], slice(0, QUARTER - scalar_cols), cols.start)
            if scalar_cols:
                group(nc.scalar.copy, y_grouped[k], y[h], slice(QUARTER - scalar_cols, QUARTER), cols.start)

        def store_codes(h):
            nc.sync.dma_start(out=y_words[:, halves[h]], in_=y_codes[h][:].bitcast(I32))

        for t in range(LAST):
            gather_and_turn(t)
            group_values(t)
            if t:
                quantize_values(t - 1)
        gather_and_turn(LAST)

        round_weights(0)
        quantize_weights(0)
        round_weights(1)
        group_values(LAST)
        quantize_values(2)
        quantize_weights(1)
        quantize_values(LAST)
        for k in (2, 3):
            round_weights(k)
            quantize_weights(k)

        multiply(0, 0, left)
        store_results(0, slice(0, 1), left)
        for t in range(1, LAST):
            multiply(t, 0, left)
        store_results(0, slice(1, LAST), left)
        for t in range(LAST):
            multiply(t, 0, right)
        store_results(0, slice(0, LAST), right)
        multiply(LAST, 0, whole)
        store_results(0, slice(LAST, PACK), whole)
        for cols in (left, right):
            round_results(0, cols)
        for cols in (left, right):
            quantize_results(0, cols)

        for t in range(PACK):
            multiply(t, 1, left)
        store_results(1, slice(0, PACK), left)
        store_codes(0)
        round_results(1, left)

        for t in range(PACK):
            multiply(t, 1, right)
        store_results(1, slice(0, PACK), right)
        round_results(1, right, SCALAR_RESULT_COLS)
        for cols in (left, right):
            quantize_results(1, cols)
        store_codes(1)

        for quad in range(P // 32):
            queue = nc.scalar if quad % 2 == 0 else nc.sync
            queue.dma_start(
                out=y_scale_rows[4 * quad : 4 * quad + 4, :],
                in_=y_scales[32 * quad : 32 * quad + 4, :].bitcast(I32),
            )
